import numpy as np
import ml_dtypes


def mxq(x, axis, fmt="e4m3"):
    dtype, down = {"e4m3": (ml_dtypes.float8_e4m3fn, 7), "e5m2": (ml_dtypes.float8_e5m2, 14)}[fmt]
    v = np.moveaxis(np.asarray(x, np.float32).astype(ml_dtypes.bfloat16).astype(np.float64), axis, -1)
    blocks = v.reshape(v.shape[:-1] + (-1, 32))
    amax = np.abs(blocks).max(-1, keepdims=True)
    byte = np.maximum(np.where(amax > 0, np.frexp(amax)[1] - 1 + 127, 0) - down, 1)
    scale = np.exp2(byte - 127.0)
    codes = (blocks / scale).astype(np.float32).astype(dtype).astype(np.float64)
    return np.moveaxis((codes * scale).reshape(v.shape), -1, axis)


WIDE = False


def mx_kscale(k):
    if not WIDE:
        return np.ones(k)
    levels = np.array([18, -18])
    if k % 512:
        return np.exp2(np.random.permutation(np.resize(levels, k // 32))).repeat(32)
    a = np.empty((k // 512, 16))
    for p in range(k // 512):
        a[p, :8] = np.random.permutation(np.resize(levels, 8))
        for g in range(8):
            far = levels[np.abs(levels - a[p, g]) >= 10]
            a[p, g + 8] = far[np.random.randint(len(far))]
    return np.exp2(a.ravel()).repeat(32)


def f64(x):
    return np.asarray(x).astype(np.float64)


def striped(idx):
    return np.tile(np.asarray(idx).reshape(-1, 16).T, (8, 1)).astype(np.uint16)


def unstriped(offs):
    return offs[:16].T.reshape(-1).astype(np.int64)

def planes(y):
    n, m = y.shape
    v = y.astype(np.float32).astype(ml_dtypes.bfloat16).astype(np.float64).reshape(n // 32, 32, m)
    top = np.abs(v).max(1)
    byte = np.clip(np.where(top > 0, np.frexp(top)[1] - 1 + 127 - 7, 1), 1, 254)
    codes = (v * np.exp2(127.0 - byte)[:, None, :]).reshape(n, m).astype(np.float32).astype(ml_dtypes.float8_e4m3fn).view(np.uint8)
    words = codes.reshape(n // 512, 128, 4, m).transpose(0, 1, 3, 2)
    return np.ascontiguousarray(words), np.ascontiguousarray(byte.astype(np.uint8).reshape(n // 512, 16, m))


def setup_inputs():
    n = np.random.standard_normal
    uni = np.random.uniform
    idx = np.random.permutation(2048)[:512]
    f_f = mx_kscale(512)
    return {
        "dy": (np.round(n((512, 512)) * 8) / 8 * f_f[:, None]).astype(np.float32),
        "x": (np.round(n((512, 512)) * 8) / 8).astype(np.float32),
        "wg": (n((512, 512)) / np.sqrt(512) / f_f[:, None]).astype(np.float32),
        "wb": (n((512, 512)) / np.sqrt(512) / f_f[:, None]).astype(np.float32),
        "offs": striped(idx),
    }


def reference(dy, x, wg, wb, offs):
    idx = unstriped(offs)
    dg = f64(dy) * f64(x)
    c1 = mxq(f64(wg), 0, "e4m3").T @ mxq(dg, 0, "e5m2")
    c2 = mxq(f64(wb), 0, "e4m3").T @ mxq(f64(dy), 0, "e5m2")
    dc = c1 + c2
    out_0 = np.zeros((512, 2048))
    out_0[:, idx] = dc
    return (out_0,) + planes(out_0)

@@ -1,0 +1,153 @@
+from contextlib import ExitStack
+
+import concourse.mybir as mybir
+
+F = 512
+D = 512
+N = 512
+T = 2048
+
+FLOPS = 2 * 2 * F * D * N
+
+F32 = mybir.dt.float32
+BF16 = mybir.dt.bfloat16
+I32 = mybir.dt.int32
+U32 = mybir.dt.uint32
+U16 = mybir.dt.uint16
+U8 = mybir.dt.uint8
+E4M3 = mybir.dt.float8_e4m3fn_x4
+E5M2 = mybir.dt.float8_e5m2_x4
+
+P = 128
+LANES = 4
+RUN = 4
+CHUNKS = (256, 256, 512, 512, 512)
+
+
+def tile_attend_gfilm_c_pl_kernel(tc, dy, x, wg, wb, offs, out_0, out_1, out_2):
+    nc = tc.nc
+    with ExitStack() as ctx:
+        sb = ctx.enter_context(tc.tile_pool(name="sb", bufs=1))
+        psum = ctx.enter_context(tc.psum_pool(name="psum", bufs=1))
+
+        def load(src, name):
+            raw = sb.tile([P, LANES, src.shape[1]], F32, name=name)
+            nc.sync.dma_start(out=raw[:], in_=src.rearrange("(p j) c -> p j c", j=LANES))
+            return raw
+
+        dy_raw = load(dy, "dy_raw")
+        x_raw = load(x, "x_raw")
+        wg_raw = load(wg, "wg_raw")
+        wb_raw = load(wb, "wb_raw")
+        offsets = sb.tile([P, N // 16], U16, name="offsets")
+        nc.sync.dma_start(offsets[:], offs)
+
+        windows = []
+        for t in range(LANES):
+            window = sb.tile([P, T], F32, name="window%d" % t)
+            nc.vector.memset(window[:].bitcast(I32), 0)
+            windows.append(window)
+
+        def runs(raw, cols):
+            return raw[:, :, cols].rearrange("p j (c i) -> p c j i", i=RUN)
+
+        def woven(tile, cols):
+            view = tile[:].rearrange("p (c j) -> p c j", j=LANES)[:, cols, :]
+            return view.rearrange("p (c i) j -> p c j i", i=RUN)
+
+        def quantize(values, fmt, name):
+            words = values.shape[1] // LANES
+            codes = sb.tile([P, words], U32, name=name + "_codes", align_bytes=64)
+            scales = sb.tile([P, words], U8, name=name + "_scales", align_bytes=64)
+            nc.vector.quantize_mx(out=codes[:].bitcast(fmt), scales=scales[:], in_=values)
+            return codes, scales
+
+        dy_bf = sb.tile([P, N * LANES], BF16, name="dy_bf", align_bytes=64)
+        dg_bf = sb.tile([P, N * LANES], BF16, name="dg_bf", align_bytes=64)
+        lo, hi = slice(0, N // 2), slice(N // 2, N)
+        nc.scalar.copy(out=woven(dy_bf, lo), in_=runs(dy_raw, lo))
+        nc.vector.tensor_copy(out=woven(dy_bf, hi), in_=runs(dy_raw, hi))
+        dy_mx = quantize(dy_bf[:], E5M2, "dy")
+        every = slice(0, N)
+        nc.vector.tensor_tensor(out=woven(dg_bf, every), in0=runs(dy_raw, every), in1=runs(x_raw, every),
+                                op=mybir.AluOpType.mult)
+        dg_mx = quantize(dg_bf[:], E5M2, "dg")
+
+        half = 2 * P * LANES
+
+        def dealt_out(values):
+            return values.rearrange("p (t m j) -> p m j t", t=2, j=LANES)
+
+        def dealt_in(raw, t0):
+            return raw[:].rearrange("p j (m t) -> p m j t", t=LANES)[:, :, :, t0:t0 + 2]
+
+        wg01_bf = sb.tile([P, half], BF16, name="wg01_bf", align_bytes=64)
+        wb01_bf = sb.tile([P, half], BF16, name="wb01_bf", align_bytes=64)
+        w23_bf = sb.tile([P, 2 * half], BF16, name="w23_bf", align_bytes=64)
+        nc.scalar.copy(out=dealt_out(w23_bf[:, :half]), in_=dealt_in(wg_raw, 2))
+        nc.vector.tensor_copy(out=dealt_out(wg01_bf[:]), in_=dealt_in(wg_raw, 0))
+        wg01_mx = quantize(wg01_bf[:], E4M3, "wg01")
+        nc.vector.tensor_copy(out=dealt_out(wb01_bf[:]), in_=dealt_in(wb_raw, 0))
+        nc.scalar.copy(out=dealt_out(w23_bf[:, half:]), in_=dealt_in(wb_raw, 2))
+        wb01_mx = quantize(wb01_bf[:], E4M3, "wb01")
+        w23_mx = quantize(w23_bf[:], E4M3, "w23")
+        gains = [(wg01_mx, 0), (wg01_mx, 1), (w23_mx, 0), (w23_mx, 1)]
+        shifts = [(wb01_mx, 0), (wb01_mx, 1), (w23_mx, 2), (w23_mx, 3)]
+
+        def mx_pass(acc, weights, moving, start):
+            (codes, scales), block = weights
+            cols = slice(block * P, (block + 1) * P)
+            nc.tensor.matmul_mx(out=acc[:], lhsT=codes[:, cols].bitcast(E4M3), lhsT_scale=scales[:, cols],
+                                rhs=moving[0][:].bitcast(E5M2), rhs_scale=moving[1][:],
+                                start=start, stop=not start)
+
+        dense = []
+        for t in range(LANES):
+            acc = psum.tile([P, N], F32, name="acc%d" % t)
+            mx_pass(acc, gains[t], dg_mx, True)
+            mx_pass(acc, shifts[t], dy_mx, False)
+            sums = sb.tile([P, N], F32, name="sums%d" % t)
+            nc.scalar.copy(out=sums[:], in_=acc[:])
+            dense.append(sums)
+
+        starts = [sum(CHUNKS[:k]) for k in range(len(CHUNKS))]
+        pairs = [sb.tile([P, 2, w, 2], BF16, name="pairs%d" % k) for k, w in enumerate(CHUNKS)]
+        out_rows = out_0.rearrange("(p t) c -> p t c", t=LANES)
+        for t in range(LANES):
+            nc.vector.tensor_copy(out=windows[t][:].indirect(offsets[:]), in_=dense[t][:])
+            nc.sync.dma_start(out=out_rows[:, t, :], in_=windows[t][:])
+            for k, w in enumerate(CHUNKS):
+                nc.scalar.copy(out=pairs[k][:, t // 2, :, t % 2], in_=windows[t][:, starts[k]:starts[k] + w])
+
+        out_words = out_1.rearrange("a p c l -> p (a c l)").bitcast(I32)
+        out_scales = out_2.rearrange("a q c -> (a q) c").bitcast(I32)
+        y_scales = sb.tile([P, T], U8, name="y_scales", align_bytes=64)
+        last = len(CHUNKS) - 1
+        y_bf = []
+
+        def weave(k):
+            w = CHUNKS[k]
+            tile = sb.tile([P, w * LANES], BF16, name="y_bf%d" % k, align_bytes=64)
+            view = U32 if k == last else I32
+            src = pairs[k][:].rearrange("p u c e -> p (u c e)").bitcast(view).rearrange("p (u c) -> p c u", u=2)
+            dst = tile[:].bitcast(view).rearrange("p (c u) -> p c u", u=2)
+            if k == last:
+                nc.scalar.copy(out=dst, in_=src)
+            else:
+                nc.vector.tensor_copy(out=dst, in_=src)
+            y_bf.append(tile)
+
+        def planes(k):
+            cols = slice(starts[k], starts[k] + CHUNKS[k])
+            codes = sb.tile([P, CHUNKS[k]], U32, name="y_codes%d" % k, align_bytes=64)
+            nc.vector.quantize_mx(out=codes[:].bitcast(E4M3), scales=y_scales[:, cols], in_=y_bf[k][:])
+            nc.sync.dma_start(out=out_words[:, cols], in_=codes[:].bitcast(I32))
+
+        weave(0)
+        for k in range(1, len(CHUNKS)):
+            weave(k)
+            planes(k - 1)
+        planes(last)
+        for q in range(4):
+            queue = nc.sync if q % 2 == 0 else nc.scalar
+            queue.dma_start(out=out_scales[4 * q:4 * q + 4, :], in_=y_scales[32 * q:32 * q + 4, :].bitcast(I32))

@@ -21,7 +21,9 @@ E5M2 = mybir.dt.float8_e5m2_x4
 P = 128
 LANES = 4
 RUN = 4
-CHUNKS = (256, 256, 512, 512, 512)
+CHUNKS = (256, 512, 512, 256, 256, 256)
+VECTOR_CHUNKS = 3
+M_VECTOR = 84
 
 
 def tile_attend_gfilm_c_pl_kernel(tc, dy, x, wg, wb, offs, out_0, out_1, out_2):
@@ -43,7 +45,7 @@ def tile_attend_gfilm_c_pl_kernel(tc, dy, x, wg, wb, offs, out_0, out_1, out_2):
         nc.sync.dma_start(offsets[:], offs)
 
         windows = []
-        for t in range(LANES):
+        for t in range(2):
             window = sb.tile([P, T], F32, name="window%d" % t)
             nc.vector.memset(window[:].bitcast(I32), 0)
             windows.append(window)
@@ -57,7 +59,7 @@ def tile_attend_gfilm_c_pl_kernel(tc, dy, x, wg, wb, offs, out_0, out_1, out_2):
 
         def quantize(values, fmt, name):
             words = values.shape[1] // LANES
-            codes = sb.tile([P, words], U32, name=name + "_codes", align_bytes=64)
+            codes = sb.tile([P, words], U32, name=name + "_codes", tag=name + "_codes", align_bytes=64)
             scales = sb.tile([P, words], U8, name=name + "_scales", align_bytes=64)
             nc.vector.quantize_mx(out=codes[:].bitcast(fmt), scales=scales[:], in_=values)
             return codes, scales
@@ -83,13 +85,15 @@ def tile_attend_gfilm_c_pl_kernel(tc, dy, x, wg, wb, offs, out_0, out_1, out_2):
 
         wg01_bf = sb.tile([P, half], BF16, name="wg01_bf", align_bytes=64)
         wb01_bf = sb.tile([P, half], BF16, name="wb01_bf", align_bytes=64)
-        w23_bf = sb.tile([P, 2 * half], BF16, name="w23_bf", align_bytes=64)
+        w23_bf = sb.tile([P, 2 * half], BF16, name="w23_bf", tag="w23_bf", align_bytes=64)
         nc.scalar.copy(out=dealt_out(w23_bf[:, :half]), in_=dealt_in(wg_raw, 2))
         nc.vector.tensor_copy(out=dealt_out(wg01_bf[:]), in_=dealt_in(wg_raw, 0))
         wg01_mx = quantize(wg01_bf[:], E4M3, "wg01")
-        nc.vector.tensor_copy(out=dealt_out(wb01_bf[:]), in_=dealt_in(wb_raw, 0))
-        nc.scalar.copy(out=dealt_out(w23_bf[:, half:]), in_=dealt_in(wb_raw, 2))
+        nc.vector.tensor_copy(out=dealt_out(wb01_bf[:])[:, :M_VECTOR], in_=dealt_in(wb_raw, 0)[:, :M_VECTOR])
+        nc.scalar.copy(out=dealt_out(wb01_bf[:])[:, M_VECTOR:], in_=dealt_in(wb_raw, 0)[:, M_VECTOR:])
         wb01_mx = quantize(wb01_bf[:], E4M3, "wb01")
+        nc.vector.tensor_copy(out=dealt_out(w23_bf[:, half:])[:, :P // 2], in_=dealt_in(wb_raw, 2)[:, :P // 2])
+        nc.scalar.copy(out=dealt_out(w23_bf[:, half:])[:, P // 2:], in_=dealt_in(wb_raw, 2)[:, P // 2:])
         w23_mx = quantize(w23_bf[:], E4M3, "w23")
         gains = [(wg01_mx, 0), (wg01_mx, 1), (w23_mx, 0), (w23_mx, 1)]
         shifts = [(wb01_mx, 0), (wb01_mx, 1), (w23_mx, 2), (w23_mx, 3)]
@@ -110,44 +114,52 @@ def tile_attend_gfilm_c_pl_kernel(tc, dy, x, wg, wb, offs, out_0, out_1, out_2):
             nc.scalar.copy(out=sums[:], in_=acc[:])
             dense.append(sums)
 
-        starts = [sum(CHUNKS[:k]) for k in range(len(CHUNKS))]
-        pairs = [sb.tile([P, 2, w, 2], BF16, name="pairs%d" % k) for k, w in enumerate(CHUNKS)]
+        for t, tag in ((2, "w23_bf"), (3, "dy_codes")):
+            window = sb.tile([P, T], F32, name="window%d" % t, tag=tag, align_bytes=64)
+            nc.gpsimd.memset(window[:], 0.0)
+            windows.append(window)
+
+        spans = [slice(sum(CHUNKS[:k]), sum(CHUNKS[:k + 1])) for k in range(len(CHUNKS))]
+        rounded = [sb.tile([P, LANES, w], BF16, name="rounded%d" % k) for k, w in enumerate(CHUNKS)]
         out_rows = out_0.rearrange("(p t) c -> p t c", t=LANES)
         for t in range(LANES):
             nc.vector.tensor_copy(out=windows[t][:].indirect(offsets[:]), in_=dense[t][:])
             nc.sync.dma_start(out=out_rows[:, t, :], in_=windows[t][:])
-            for k, w in enumerate(CHUNKS):
-                nc.scalar.copy(out=pairs[k][:, t // 2, :, t % 2], in_=windows[t][:, starts[k]:starts[k] + w])
+            for k, cols in enumerate(spans):
+                nc.scalar.copy(out=rounded[k][:, t, :], in_=windows[t][:, cols])
 
         out_words = out_1.rearrange("a p c l -> p (a c l)").bitcast(I32)
-        out_scales = out_2.rearrange("a q c -> (a q) c").bitcast(I32)
+        out_scales = out_2.rearrange("a q c -> (a q) c")
         y_scales = sb.tile([P, T], U8, name="y_scales", align_bytes=64)
-        last = len(CHUNKS) - 1
-        y_bf = []
+        y_bf = [sb.tile([P, w * LANES], BF16, name="y_bf%d" % k, align_bytes=64) for k, w in enumerate(CHUNKS)]
 
         def weave(k):
-            w = CHUNKS[k]
-            tile = sb.tile([P, w * LANES], BF16, name="y_bf%d" % k, align_bytes=64)
-            view = U32 if k == last else I32
-            src = pairs[k][:].rearrange("p u c e -> p (u c e)").bitcast(view).rearrange("p (u c) -> p c u", u=2)
-            dst = tile[:].bitcast(view).rearrange("p (c u) -> p c u", u=2)
-            if k == last:
-                nc.scalar.copy(out=dst, in_=src)
+            whole = slice(0, CHUNKS[k])
+            if k < VECTOR_CHUNKS:
+                nc.vector.tensor_copy(out=woven(y_bf[k], whole), in_=runs(rounded[k], whole))
             else:
-                nc.vector.tensor_copy(out=dst, in_=src)
-            y_bf.append(tile)
+                nc.scalar.copy(out=woven(y_bf[k], whole), in_=runs(rounded[k], whole))
 
         def planes(k):
-            cols = slice(starts[k], starts[k] + CHUNKS[k])
             codes = sb.tile([P, CHUNKS[k]], U32, name="y_codes%d" % k, align_bytes=64)
-            nc.vector.quantize_mx(out=codes[:].bitcast(E4M3), scales=y_scales[:, cols], in_=y_bf[k][:])
-            nc.sync.dma_start(out=out_words[:, cols], in_=codes[:].bitcast(I32))
+            nc.vector.quantize_mx(out=codes[:].bitcast(E4M3), scales=y_scales[:, spans[k]], in_=y_bf[k][:])
+            nc.sync.dma_start(out=out_words[:, spans[k]], in_=codes[:].bitcast(I32))
 
-        weave(0)
-        for k in range(1, len(CHUNKS)):
+        def store_scales(cols, queues):
+            for q in range(4):
+                queues[q % 2].dma_start(out=out_scales[4 * q:4 * q + 4, cols].bitcast(I32),
+                                        in_=y_scales[32 * q:32 * q + 4, cols].bitcast(I32))
+
+        for k in range(VECTOR_CHUNKS, len(CHUNKS)):
             weave(k)
-            planes(k - 1)
-        planes(last)
-        for q in range(4):
-            queue = nc.sync if q % 2 == 0 else nc.scalar
-            queue.dma_start(out=out_scales[4 * q:4 * q + 4, :], in_=y_scales[32 * q:32 * q + 4, :].bitcast(I32))
+        weave(0)
+        weave(1)
+        planes(0)
+        weave(2)
+        planes(1)
+        planes(3)
+        planes(2)
+        store_scales(slice(0, spans[3].stop), (nc.sync, nc.sync))
+        planes(4)
+        planes(5)
+        store_scales(slice(spans[3].stop, T), (nc.scalar, nc.sync))

@@ -21,13 +21,16 @@ E5M2 = mybir.dt.float8_e5m2_x4
 P = 128
 LANES = 4
 RUN = 4
-CHUNKS = (256, 512, 512, 256, 256, 256)
-VECTOR_CHUNKS = 3
-M_VECTOR = 84
+CHUNKS = ((256, False, "vector"), (256, False, "vector"), (512, True, "vector"), (128, True, "vector"),
+          (256, True, "scalar"), (256, True, "scalar"), (256, True, "scalar"), (128, True, "scalar"))
+STORE_AFTER = {1: 0, 3: 2, 5: 4, 7: 6}
+M_FIRST = 72
+M_SECOND = 48
 
 
 def tile_attend_gfilm_c_pl_kernel(tc, dy, x, wg, wb, offs, out_0, out_1, out_2):
     nc = tc.nc
+    copy = {"vector": nc.vector.tensor_copy, "scalar": nc.scalar.copy}
     with ExitStack() as ctx:
         sb = ctx.enter_context(tc.tile_pool(name="sb", bufs=1))
         psum = ctx.enter_context(tc.psum_pool(name="psum", bufs=1))
@@ -50,116 +53,123 @@ def tile_attend_gfilm_c_pl_kernel(tc, dy, x, wg, wb, offs, out_0, out_1, out_2):
             nc.vector.memset(window[:].bitcast(I32), 0)
             windows.append(window)
 
-        def runs(raw, cols):
-            return raw[:, :, cols].rearrange("p j (c i) -> p c j i", i=RUN)
+        def runs(rows):
+            return rows.rearrange("p j (c i) -> p c j i", i=RUN)
 
-        def woven(tile, cols):
-            view = tile[:].rearrange("p (c j) -> p c j", j=LANES)[:, cols, :]
-            return view.rearrange("p (c i) j -> p c j i", i=RUN)
+        def woven(values):
+            return values.rearrange("p (c i j) -> p c j i", i=RUN, j=LANES)
 
-        def quantize(values, fmt, name):
-            words = values.shape[1] // LANES
+        def mx_tiles(words, name):
             codes = sb.tile([P, words], U32, name=name + "_codes", tag=name + "_codes", align_bytes=64)
             scales = sb.tile([P, words], U8, name=name + "_scales", align_bytes=64)
-            nc.vector.quantize_mx(out=codes[:].bitcast(fmt), scales=scales[:], in_=values)
             return codes, scales
+
+        def quantize(mx, values, fmt, c0, c1):
+            nc.vector.quantize_mx(out=mx[0][:, c0:c1].bitcast(fmt), scales=mx[1][:, c0:c1],
+                                  in_=values[:, LANES * c0:LANES * c1])
 
         dy_bf = sb.tile([P, N * LANES], BF16, name="dy_bf", align_bytes=64)
         dg_bf = sb.tile([P, N * LANES], BF16, name="dg_bf", align_bytes=64)
-        lo, hi = slice(0, N // 2), slice(N // 2, N)
-        nc.scalar.copy(out=woven(dy_bf, lo), in_=runs(dy_raw, lo))
-        nc.vector.tensor_copy(out=woven(dy_bf, hi), in_=runs(dy_raw, hi))
-        dy_mx = quantize(dy_bf[:], E5M2, "dy")
-        every = slice(0, N)
-        nc.vector.tensor_tensor(out=woven(dg_bf, every), in0=runs(dy_raw, every), in1=runs(x_raw, every),
+        dy_mx = mx_tiles(N, "dy")
+        dg_mx = mx_tiles(N, "dg")
+        half = N // 2
+        nc.scalar.copy(out=woven(dy_bf[:, :LANES * half]), in_=runs(dy_raw[:, :, :half]))
+        nc.vector.tensor_copy(out=woven(dy_bf[:, LANES * half:]), in_=runs(dy_raw[:, :, half:]))
+        quantize(dy_mx, dy_bf, E5M2, 0, N)
+        nc.vector.tensor_tensor(out=woven(dg_bf[:]), in0=runs(dy_raw[:]), in1=runs(x_raw[:]),
                                 op=mybir.AluOpType.mult)
-        dg_mx = quantize(dg_bf[:], E5M2, "dg")
+        quantize(dg_mx, dg_bf, E5M2, 0, N)
 
-        half = 2 * P * LANES
+        w_bf = sb.tile([P, 2 * D * LANES], BF16, name="w_bf", align_bytes=64)
+        w_mx = mx_tiles(2 * D, "w")
+        dealt = w_bf[:].rearrange("p (t s m j) -> p s m j t", t=LANES, s=2, j=LANES)
 
-        def dealt_out(values):
-            return values.rearrange("p (t m j) -> p m j t", t=2, j=LANES)
+        def deal(engine, raw, s, t0, m0, m1):
+            src = raw[:].rearrange("p j (m t) -> p m j t", t=LANES)
+            copy[engine](out=dealt[:, s, m0:m1, :, t0:t0 + 2], in_=src[:, m0:m1, :, t0:t0 + 2])
 
-        def dealt_in(raw, t0):
-            return raw[:].rearrange("p j (m t) -> p m j t", t=LANES)[:, :, :, t0:t0 + 2]
-
-        wg01_bf = sb.tile([P, half], BF16, name="wg01_bf", align_bytes=64)
-        wb01_bf = sb.tile([P, half], BF16, name="wb01_bf", align_bytes=64)
-        w23_bf = sb.tile([P, 2 * half], BF16, name="w23_bf", tag="w23_bf", align_bytes=64)
-        nc.scalar.copy(out=dealt_out(w23_bf[:, :half]), in_=dealt_in(wg_raw, 2))
-        nc.vector.tensor_copy(out=dealt_out(wg01_bf[:]), in_=dealt_in(wg_raw, 0))
-        wg01_mx = quantize(wg01_bf[:], E4M3, "wg01")
-        nc.vector.tensor_copy(out=dealt_out(wb01_bf[:])[:, :M_VECTOR], in_=dealt_in(wb_raw, 0)[:, :M_VECTOR])
-        nc.scalar.copy(out=dealt_out(wb01_bf[:])[:, M_VECTOR:], in_=dealt_in(wb_raw, 0)[:, M_VECTOR:])
-        wb01_mx = quantize(wb01_bf[:], E4M3, "wb01")
-        nc.vector.tensor_copy(out=dealt_out(w23_bf[:, half:])[:, :P // 2], in_=dealt_in(wb_raw, 2)[:, :P // 2])
-        nc.scalar.copy(out=dealt_out(w23_bf[:, half:])[:, P // 2:], in_=dealt_in(wb_raw, 2)[:, P // 2:])
-        w23_mx = quantize(w23_bf[:], E4M3, "w23")
-        gains = [(wg01_mx, 0), (wg01_mx, 1), (w23_mx, 0), (w23_mx, 1)]
-        shifts = [(wb01_mx, 0), (wb01_mx, 1), (w23_mx, 2), (w23_mx, 3)]
-
-        def mx_pass(acc, weights, moving, start):
-            (codes, scales), block = weights
-            cols = slice(block * P, (block + 1) * P)
-            nc.tensor.matmul_mx(out=acc[:], lhsT=codes[:, cols].bitcast(E4M3), lhsT_scale=scales[:, cols],
-                                rhs=moving[0][:].bitcast(E5M2), rhs_scale=moving[1][:],
-                                start=start, stop=not start)
+        deal("scalar", wg_raw, 0, 0, 0, P)
+        quantize(w_mx, w_bf, E4M3, 0, P)
+        deal("vector", wg_raw, 0, 2, 0, P)
+        for t0, m in ((0, M_FIRST), (2, M_SECOND)):
+            deal("vector", wb_raw, 1, t0, 0, m)
+            deal("scalar", wb_raw, 1, t0, m, P)
+        quantize(w_mx, w_bf, E4M3, P, 2 * P)
+        quantize(w_mx, w_bf, E4M3, 2 * P, 4 * P)
+        quantize(w_mx, w_bf, E4M3, 4 * P, 8 * P)
 
         dense = []
         for t in range(LANES):
             acc = psum.tile([P, N], F32, name="acc%d" % t)
-            mx_pass(acc, gains[t], dg_mx, True)
-            mx_pass(acc, shifts[t], dy_mx, False)
+            for s, moving in enumerate((dg_mx, dy_mx)):
+                cols = slice((2 * t + s) * P, (2 * t + s + 1) * P)
+                nc.tensor.matmul_mx(out=acc[:], lhsT=w_mx[0][:, cols].bitcast(E4M3), lhsT_scale=w_mx[1][:, cols],
+                                    rhs=moving[0][:].bitcast(E5M2), rhs_scale=moving[1][:],
+                                    start=(s == 0), stop=(s == 1))
             sums = sb.tile([P, N], F32, name="sums%d" % t)
             nc.scalar.copy(out=sums[:], in_=acc[:])
             dense.append(sums)
 
-        for t, tag in ((2, "w23_bf"), (3, "dy_codes")):
+        for t, tag in ((2, "dg_codes"), (3, "dy_codes")):
             window = sb.tile([P, T], F32, name="window%d" % t, tag=tag, align_bytes=64)
             nc.gpsimd.memset(window[:], 0.0)
             windows.append(window)
 
-        spans = [slice(sum(CHUNKS[:k]), sum(CHUNKS[:k + 1])) for k in range(len(CHUNKS))]
-        rounded = [sb.tile([P, LANES, w], BF16, name="rounded%d" % k) for k, w in enumerate(CHUNKS)]
+        edges = [sum(chunk[0] for chunk in CHUNKS[:k]) for k in range(len(CHUNKS) + 1)]
+        rounded = [sb.tile([P, LANES * chunk[0]], BF16, name="rounded%d" % k) for k, chunk in enumerate(CHUNKS)]
+        y_bf = sb.tile([P, T * LANES], BF16, name="y_bf", align_bytes=64)
+        y_mx = mx_tiles(T, "y")
+
+        def round_lane(t, k):
+            paired = CHUNKS[k][1]
+            src = windows[t][:, edges[k]:edges[k + 1]]
+            if paired:
+                dst = rounded[k][:].rearrange("p (u c e) -> p u c e", u=2, e=2)[:, t // 2, :, t % 2]
+            else:
+                dst = rounded[k][:].rearrange("p (j c) -> p j c", j=LANES)[:, t, :]
+            copy["vector" if t == LANES - 1 and not paired else "scalar"](out=dst, in_=src)
+
+        def weave(k):
+            paired, engine = CHUNKS[k][1:]
+            dst = y_bf[:, LANES * edges[k]:LANES * edges[k + 1]]
+            if paired:
+                word = I32 if engine == "vector" else U32
+                copy[engine](out=dst.bitcast(word).rearrange("p (c u) -> p c u", u=2),
+                             in_=rounded[k][:].bitcast(word).rearrange("p (u c) -> p c u", u=2))
+            else:
+                copy[engine](out=woven(dst), in_=runs(rounded[k][:].rearrange("p (j c) -> p j c", j=LANES)))
+
+        out_words = out_1.rearrange("a p c l -> p (a c l)").bitcast(I32)
+
+        def planes(k):
+            quantize(y_mx, y_bf, E4M3, edges[k], edges[k + 1])
+            if k in STORE_AFTER:
+                first = edges[STORE_AFTER[k]]
+                nc.sync.dma_start(out=out_words[:, first:edges[k + 1]],
+                                  in_=y_mx[0][:, first:edges[k + 1]].bitcast(I32))
+
         out_rows = out_0.rearrange("(p t) c -> p t c", t=LANES)
         for t in range(LANES):
             nc.vector.tensor_copy(out=windows[t][:].indirect(offsets[:]), in_=dense[t][:])
             nc.sync.dma_start(out=out_rows[:, t, :], in_=windows[t][:])
-            for k, cols in enumerate(spans):
-                nc.scalar.copy(out=rounded[k][:, t, :], in_=windows[t][:, cols])
+            if t < LANES - 1:
+                for k in range(len(CHUNKS)):
+                    round_lane(t, k)
 
-        out_words = out_1.rearrange("a p c l -> p (a c l)").bitcast(I32)
-        out_scales = out_2.rearrange("a q c -> (a q) c")
-        y_scales = sb.tile([P, T], U8, name="y_scales", align_bytes=64)
-        y_bf = [sb.tile([P, w * LANES], BF16, name="y_bf%d" % k, align_bytes=64) for k, w in enumerate(CHUNKS)]
-
-        def weave(k):
-            whole = slice(0, CHUNKS[k])
-            if k < VECTOR_CHUNKS:
-                nc.vector.tensor_copy(out=woven(y_bf[k], whole), in_=runs(rounded[k], whole))
-            else:
-                nc.scalar.copy(out=woven(y_bf[k], whole), in_=runs(rounded[k], whole))
-
-        def planes(k):
-            codes = sb.tile([P, CHUNKS[k]], U32, name="y_codes%d" % k, align_bytes=64)
-            nc.vector.quantize_mx(out=codes[:].bitcast(E4M3), scales=y_scales[:, spans[k]], in_=y_bf[k][:])
-            nc.sync.dma_start(out=out_words[:, spans[k]], in_=codes[:].bitcast(I32))
-
-        def store_scales(cols, queues):
-            for q in range(4):
-                queues[q % 2].dma_start(out=out_scales[4 * q:4 * q + 4, cols].bitcast(I32),
-                                        in_=y_scales[32 * q:32 * q + 4, cols].bitcast(I32))
-
-        for k in range(VECTOR_CHUNKS, len(CHUNKS)):
-            weave(k)
+        last = LANES - 1
+        for k in range(5):
+            round_lane(last, k)
+        for k in range(5, len(CHUNKS)):
+            round_lane(last, k)
+            weave(k - 1)
+        weave(len(CHUNKS) - 1)
         weave(0)
-        weave(1)
-        planes(0)
-        weave(2)
-        planes(1)
-        planes(3)
-        planes(2)
-        store_scales(slice(0, spans[3].stop), (nc.sync, nc.sync))
-        planes(4)
-        planes(5)
-        store_scales(slice(spans[3].stop, T), (nc.scalar, nc.sync))
+        for k in range(1, 4):
+            weave(k)
+            planes(k - 1)
+        for k in range(3, len(CHUNKS)):
+            planes(k)
+        out_scales = out_2.rearrange("a q c -> (a q) c").bitcast(I32)
+        for q in range(4):
+            queue = nc.scalar if q % 2 == 0 else nc.sync
+            queue.dma_start(out=out_scales[4 * q:4 * q + 4, :], in_=y_mx[1][32 * q:32 * q + 4, :].bitcast(I32))

@@ -21,11 +21,16 @@ E5M2 = mybir.dt.float8_e5m2_x4
 P = 128
 LANES = 4
 RUN = 4
+
+DY_SCALAR = 384
+WG_LATE_VECTOR = 64
+WB_EARLY_VECTOR = 72
+WB_LATE_VECTOR = 48
+CLEAR = 512
+
 CHUNKS = ((256, False, "vector"), (256, False, "vector"), (512, True, "vector"), (128, True, "vector"),
           (256, True, "scalar"), (256, True, "scalar"), (256, True, "scalar"), (128, True, "scalar"))
-STORE_AFTER = {1: 0, 3: 2, 5: 4, 7: 6}
-M_FIRST = 72
-M_SECOND = 48
+VECTOR_CHUNKS = 4
 
 
 def tile_attend_gfilm_c_pl_kernel(tc, dy, x, wg, wb, offs, out_0, out_1, out_2):
@@ -60,7 +65,7 @@ def tile_attend_gfilm_c_pl_kernel(tc, dy, x, wg, wb, offs, out_0, out_1, out_2):
             return values.rearrange("p (c i j) -> p c j i", i=RUN, j=LANES)
 
         def mx_tiles(words, name):
-            codes = sb.tile([P, words], U32, name=name + "_codes", tag=name + "_codes", align_bytes=64)
+            codes = sb.tile([P, words], U32, name=name + "_codes", align_bytes=64)
             scales = sb.tile([P, words], U8, name=name + "_scales", align_bytes=64)
             return codes, scales
 
@@ -72,9 +77,8 @@ def tile_attend_gfilm_c_pl_kernel(tc, dy, x, wg, wb, offs, out_0, out_1, out_2):
         dg_bf = sb.tile([P, N * LANES], BF16, name="dg_bf", align_bytes=64)
         dy_mx = mx_tiles(N, "dy")
         dg_mx = mx_tiles(N, "dg")
-        half = N // 2
-        nc.scalar.copy(out=woven(dy_bf[:, :LANES * half]), in_=runs(dy_raw[:, :, :half]))
-        nc.vector.tensor_copy(out=woven(dy_bf[:, LANES * half:]), in_=runs(dy_raw[:, :, half:]))
+        nc.scalar.copy(out=woven(dy_bf[:, :LANES * DY_SCALAR]), in_=runs(dy_raw[:, :, :DY_SCALAR]))
+        nc.vector.tensor_copy(out=woven(dy_bf[:, LANES * DY_SCALAR:]), in_=runs(dy_raw[:, :, DY_SCALAR:]))
         quantize(dy_mx, dy_bf, E5M2, 0, N)
         nc.vector.tensor_tensor(out=woven(dg_bf[:]), in0=runs(dy_raw[:]), in1=runs(x_raw[:]),
                                 op=mybir.AluOpType.mult)
@@ -90,8 +94,9 @@ def tile_attend_gfilm_c_pl_kernel(tc, dy, x, wg, wb, offs, out_0, out_1, out_2):
 
         deal("scalar", wg_raw, 0, 0, 0, P)
         quantize(w_mx, w_bf, E4M3, 0, P)
-        deal("vector", wg_raw, 0, 2, 0, P)
-        for t0, m in ((0, M_FIRST), (2, M_SECOND)):
+        deal("vector", wg_raw, 0, 2, 0, WG_LATE_VECTOR)
+        deal("scalar", wg_raw, 0, 2, WG_LATE_VECTOR, P)
+        for t0, m in ((0, WB_EARLY_VECTOR), (2, WB_LATE_VECTOR)):
             deal("vector", wb_raw, 1, t0, 0, m)
             deal("scalar", wb_raw, 1, t0, m, P)
         quantize(w_mx, w_bf, E4M3, P, 2 * P)
@@ -110,15 +115,16 @@ def tile_attend_gfilm_c_pl_kernel(tc, dy, x, wg, wb, offs, out_0, out_1, out_2):
             nc.scalar.copy(out=sums[:], in_=acc[:])
             dense.append(sums)
 
-        for t, tag in ((2, "dg_codes"), (3, "dy_codes")):
-            window = sb.tile([P, T], F32, name="window%d" % t, tag=tag, align_bytes=64)
-            nc.gpsimd.memset(window[:], 0.0)
-            windows.append(window)
+        window = sb.tile([P, T], F32, name="window2")
+        for c0 in range(0, T, CLEAR):
+            nc.vector.memset(window[:, c0:c0 + CLEAR].bitcast(I32), 0)
+        windows.extend([window, windows[0]])
 
         edges = [sum(chunk[0] for chunk in CHUNKS[:k]) for k in range(len(CHUNKS) + 1)]
         rounded = [sb.tile([P, LANES * chunk[0]], BF16, name="rounded%d" % k) for k, chunk in enumerate(CHUNKS)]
         y_bf = sb.tile([P, T * LANES], BF16, name="y_bf", align_bytes=64)
         y_mx = mx_tiles(T, "y")
+        last_lane = LANES - 1
 
         def round_lane(t, k):
             paired = CHUNKS[k][1]
@@ -127,7 +133,7 @@ def tile_attend_gfilm_c_pl_kernel(tc, dy, x, wg, wb, offs, out_0, out_1, out_2):
                 dst = rounded[k][:].rearrange("p (u c e) -> p u c e", u=2, e=2)[:, t // 2, :, t % 2]
             else:
                 dst = rounded[k][:].rearrange("p (j c) -> p j c", j=LANES)[:, t, :]
-            copy["vector" if t == LANES - 1 and not paired else "scalar"](out=dst, in_=src)
+            copy["vector" if t == last_lane and not paired else "scalar"](out=dst, in_=src)
 
         def weave(k):
             paired, engine = CHUNKS[k][1:]
@@ -143,33 +149,32 @@ def tile_attend_gfilm_c_pl_kernel(tc, dy, x, wg, wb, offs, out_0, out_1, out_2):
 
         def planes(k):
             quantize(y_mx, y_bf, E4M3, edges[k], edges[k + 1])
-            if k in STORE_AFTER:
-                first = edges[STORE_AFTER[k]]
-                nc.sync.dma_start(out=out_words[:, first:edges[k + 1]],
-                                  in_=y_mx[0][:, first:edges[k + 1]].bitcast(I32))
+            if k % 2 == 1:
+                cols = slice(edges[k - 1], edges[k + 1])
+                nc.sync.dma_start(out=out_words[:, cols], in_=y_mx[0][:, cols].bitcast(I32))
 
         out_rows = out_0.rearrange("(p t) c -> p t c", t=LANES)
         for t in range(LANES):
             nc.vector.tensor_copy(out=windows[t][:].indirect(offsets[:]), in_=dense[t][:])
             nc.sync.dma_start(out=out_rows[:, t, :], in_=windows[t][:])
-            if t < LANES - 1:
+            if t < last_lane:
                 for k in range(len(CHUNKS)):
                     round_lane(t, k)
 
-        last = LANES - 1
-        for k in range(5):
-            round_lane(last, k)
-        for k in range(5, len(CHUNKS)):
-            round_lane(last, k)
+        for k in range(VECTOR_CHUNKS + 1):
+            round_lane(last_lane, k)
+        for k in range(VECTOR_CHUNKS + 1, len(CHUNKS)):
+            round_lane(last_lane, k)
             weave(k - 1)
         weave(len(CHUNKS) - 1)
         weave(0)
-        for k in range(1, 4):
+        for k in range(1, VECTOR_CHUNKS):
             weave(k)
             planes(k - 1)
-        for k in range(3, len(CHUNKS)):
+        for k in range(VECTOR_CHUNKS - 1, len(CHUNKS)):
             planes(k)
+
         out_scales = out_2.rearrange("a q c -> (a q) c").bitcast(I32)
-        for q in range(4):
+        for q in range(P // 32):
             queue = nc.scalar if q % 2 == 0 else nc.sync
             queue.dma_start(out=out_scales[4 * q:4 * q + 4, :], in_=y_mx[1][32 * q:32 * q + 4, :].bitcast(I32))

@@ -21,16 +21,17 @@ E5M2 = mybir.dt.float8_e5m2_x4
 P = 128
 LANES = 4
 RUN = 4
+ORDER = (0, 2, 3, 1)
+SPLIT = 960
+PAIRED = 128
+VECTOR_QUANT = (512, 256, 128)
 
-DY_SCALAR = 384
-WG_LATE_VECTOR = 64
-WB_EARLY_VECTOR = 72
-WB_LATE_VECTOR = 48
-CLEAR = 512
-
-CHUNKS = ((256, False, "vector"), (256, False, "vector"), (512, True, "vector"), (128, True, "vector"),
-          (256, True, "scalar"), (256, True, "scalar"), (256, True, "scalar"), (128, True, "scalar"))
-VECTOR_CHUNKS = 4
+DY_SCALAR = 192
+WG_VECTOR = 96
+WB_EARLY_VECTOR = 96
+WB_LATE_VECTOR = 64
+VECTOR_CHUNKS = (512, 448)
+SCALAR_CHUNKS = (192, 256, 256, 256)
 
 
 def tile_attend_gfilm_c_pl_kernel(tc, dy, x, wg, wb, offs, out_0, out_1, out_2):
@@ -40,23 +41,25 @@ def tile_attend_gfilm_c_pl_kernel(tc, dy, x, wg, wb, offs, out_0, out_1, out_2):
         sb = ctx.enter_context(tc.tile_pool(name="sb", bufs=1))
         psum = ctx.enter_context(tc.psum_pool(name="psum", bufs=1))
 
-        def load(src, name):
-            raw = sb.tile([P, LANES, src.shape[1]], F32, name=name)
-            nc.sync.dma_start(out=raw[:], in_=src.rearrange("(p j) c -> p j c", j=LANES))
+        def load(src, name, c0, c1):
+            raw = sb.tile([P, LANES, c1 - c0], F32, name=name)
+            nc.sync.dma_start(out=raw[:], in_=src.rearrange("(p j) c -> p j c", j=LANES)[:, :, c0:c1])
             return raw
 
-        dy_raw = load(dy, "dy_raw")
-        x_raw = load(x, "x_raw")
-        wg_raw = load(wg, "wg_raw")
-        wb_raw = load(wb, "wb_raw")
+        dy_raw = load(dy, "dy_raw", 0, N)
+        x_raw = [load(x, "x_raw%d" % h, h * N // 2, (h + 1) * N // 2) for h in range(2)]
+        wg_raw = load(wg, "wg_raw", 0, D)
+        wb_raw = load(wb, "wb_raw", 0, D)
         offsets = sb.tile([P, N // 16], U16, name="offsets")
         nc.sync.dma_start(offsets[:], offs)
 
         windows = []
-        for t in range(2):
-            window = sb.tile([P, T], F32, name="window%d" % t)
-            nc.vector.memset(window[:].bitcast(I32), 0)
+        for n in range(3):
+            window = sb.tile([P, T], F32, name="window%d" % n)
+            clear = nc.gpsimd if n == 2 else nc.vector
+            clear.memset(window[:].bitcast(I32), 0)
             windows.append(window)
+        windows.append(windows[0])
 
         def runs(rows):
             return rows.rearrange("p j (c i) -> p c j i", i=RUN)
@@ -79,102 +82,105 @@ def tile_attend_gfilm_c_pl_kernel(tc, dy, x, wg, wb, offs, out_0, out_1, out_2):
         dg_mx = mx_tiles(N, "dg")
         nc.scalar.copy(out=woven(dy_bf[:, :LANES * DY_SCALAR]), in_=runs(dy_raw[:, :, :DY_SCALAR]))
         nc.vector.tensor_copy(out=woven(dy_bf[:, LANES * DY_SCALAR:]), in_=runs(dy_raw[:, :, DY_SCALAR:]))
+        for h in range(2):
+            cols = slice(h * N // 2, (h + 1) * N // 2)
+            nc.vector.tensor_tensor(out=woven(dg_bf[:, LANES * cols.start:LANES * cols.stop]),
+                                    in0=runs(dy_raw[:, :, cols]), in1=runs(x_raw[h][:]), op=mybir.AluOpType.mult)
         quantize(dy_mx, dy_bf, E5M2, 0, N)
-        nc.vector.tensor_tensor(out=woven(dg_bf[:]), in0=runs(dy_raw[:]), in1=runs(x_raw[:]),
-                                op=mybir.AluOpType.mult)
         quantize(dg_mx, dg_bf, E5M2, 0, N)
 
-        w_bf = sb.tile([P, 2 * D * LANES], BF16, name="w_bf", align_bytes=64)
-        w_mx = mx_tiles(2 * D, "w")
-        dealt = w_bf[:].rearrange("p (t s m j) -> p s m j t", t=LANES, s=2, j=LANES)
+        w_bf = [sb.tile([P, D * LANES], BF16, name="w_bf%d" % s, align_bytes=64) for s in range(2)]
+        w_mx = [mx_tiles(D, "w%d" % s) for s in range(2)]
 
-        def deal(engine, raw, s, t0, m0, m1):
+        def deal(engine, raw, s, t0, t1, m0, m1):
+            dealt = w_bf[s][:].rearrange("p (t m j) -> p m j t", t=LANES, j=LANES)
             src = raw[:].rearrange("p j (m t) -> p m j t", t=LANES)
-            copy[engine](out=dealt[:, s, m0:m1, :, t0:t0 + 2], in_=src[:, m0:m1, :, t0:t0 + 2])
+            copy[engine](out=dealt[:, m0:m1, :, t0:t1], in_=src[:, m0:m1, :, t0:t1])
 
-        deal("scalar", wg_raw, 0, 0, 0, P)
-        quantize(w_mx, w_bf, E4M3, 0, P)
-        deal("vector", wg_raw, 0, 2, 0, WG_LATE_VECTOR)
-        deal("scalar", wg_raw, 0, 2, WG_LATE_VECTOR, P)
+        deal("scalar", wg_raw, 0, 0, LANES, WG_VECTOR, P)
+        deal("vector", wg_raw, 0, 0, LANES, 0, WG_VECTOR)
+        quantize(w_mx[0], w_bf[0], E4M3, 0, D // 2)
+        quantize(w_mx[0], w_bf[0], E4M3, D // 2, D)
         for t0, m in ((0, WB_EARLY_VECTOR), (2, WB_LATE_VECTOR)):
-            deal("vector", wb_raw, 1, t0, 0, m)
-            deal("scalar", wb_raw, 1, t0, m, P)
-        quantize(w_mx, w_bf, E4M3, P, 2 * P)
-        quantize(w_mx, w_bf, E4M3, 2 * P, 4 * P)
-        quantize(w_mx, w_bf, E4M3, 4 * P, 8 * P)
+            deal("vector", wb_raw, 1, t0, t0 + 2, 0, m)
+            deal("scalar", wb_raw, 1, t0, t0 + 2, m, P)
+            if t0 == 0:
+                quantize(w_mx[1], w_bf[1], E4M3, 0, P)
+        quantize(w_mx[1], w_bf[1], E4M3, P, 2 * P)
+        quantize(w_mx[1], w_bf[1], E4M3, 2 * P, 4 * P)
 
-        dense = []
-        for t in range(LANES):
-            acc = psum.tile([P, N], F32, name="acc%d" % t)
+        dense = {}
+        for n, t in enumerate(ORDER):
+            acc = psum.tile([P, N], F32, name="acc%d" % (n % 2))
+            cols = slice(t * P, (t + 1) * P)
             for s, moving in enumerate((dg_mx, dy_mx)):
-                cols = slice((2 * t + s) * P, (2 * t + s + 1) * P)
-                nc.tensor.matmul_mx(out=acc[:], lhsT=w_mx[0][:, cols].bitcast(E4M3), lhsT_scale=w_mx[1][:, cols],
+                nc.tensor.matmul_mx(out=acc[:], lhsT=w_mx[s][0][:, cols].bitcast(E4M3), lhsT_scale=w_mx[s][1][:, cols],
                                     rhs=moving[0][:].bitcast(E5M2), rhs_scale=moving[1][:],
                                     start=(s == 0), stop=(s == 1))
-            sums = sb.tile([P, N], F32, name="sums%d" % t)
-            nc.scalar.copy(out=sums[:], in_=acc[:])
-            dense.append(sums)
+            parts = 1 if t == ORDER[0] else 1
+            dense[t] = []
+            for h in range(parts):
+                sums = sb.tile([P, N // parts], F32, name="sums%d_%d" % (t, h))
+                nc.scalar.copy(out=sums[:], in_=acc[:, h * N // parts:(h + 1) * N // parts])
+                dense[t].append(sums)
 
-        window = sb.tile([P, T], F32, name="window2")
-        for c0 in range(0, T, CLEAR):
-            nc.vector.memset(window[:, c0:c0 + CLEAR].bitcast(I32), 0)
-        windows.extend([window, windows[0]])
-
-        edges = [sum(chunk[0] for chunk in CHUNKS[:k]) for k in range(len(CHUNKS) + 1)]
-        rounded = [sb.tile([P, LANES * chunk[0]], BF16, name="rounded%d" % k) for k, chunk in enumerate(CHUNKS)]
-        y_bf = sb.tile([P, T * LANES], BF16, name="y_bf", align_bytes=64)
+        y_bf = sb.tile([P, T * LANES], BF16, name="dy_codes", align_bytes=64)
         y_mx = mx_tiles(T, "y")
-        last_lane = LANES - 1
+        paired = sb.tile([P, LANES * PAIRED], BF16, name="dg_codes", align_bytes=64)
+        direct = T - PAIRED
+        copy["gpsimd"] = nc.gpsimd.tensor_copy
 
-        def round_lane(t, k):
-            paired = CHUNKS[k][1]
-            src = windows[t][:, edges[k]:edges[k + 1]]
-            if paired:
-                dst = rounded[k][:].rearrange("p (u c e) -> p u c e", u=2, e=2)[:, t // 2, :, t % 2]
-            else:
-                dst = rounded[k][:].rearrange("p (j c) -> p j c", j=LANES)[:, t, :]
-            copy["vector" if t == last_lane and not paired else "scalar"](out=dst, in_=src)
+        def place(engine, n, c0, c1):
+            dst = y_bf[:, LANES * c0:LANES * c1].rearrange("p (c t) -> p t c", t=LANES)[:, ORDER[n], :]
+            copy[engine](out=dst, in_=windows[n][:, c0:c1])
 
-        def weave(k):
-            paired, engine = CHUNKS[k][1:]
-            dst = y_bf[:, LANES * edges[k]:LANES * edges[k + 1]]
-            if paired:
-                word = I32 if engine == "vector" else U32
-                copy[engine](out=dst.bitcast(word).rearrange("p (c u) -> p c u", u=2),
-                             in_=rounded[k][:].bitcast(word).rearrange("p (u c) -> p c u", u=2))
-            else:
-                copy[engine](out=woven(dst), in_=runs(rounded[k][:].rearrange("p (j c) -> p j c", j=LANES)))
+        def pair(n):
+            t = ORDER[n]
+            dst = paired[:].rearrange("p (u c e) -> p u e c", u=2, e=2)[:, t // 2, t % 2, :]
+            nc.scalar.copy(out=dst, in_=windows[n][:, direct:])
 
         out_words = out_1.rearrange("a p c l -> p (a c l)").bitcast(I32)
+        out_scales = out_2.rearrange("a q c -> (a q) c").bitcast(I32)
 
-        def planes(k):
-            quantize(y_mx, y_bf, E4M3, edges[k], edges[k + 1])
-            if k % 2 == 1:
-                cols = slice(edges[k - 1], edges[k + 1])
-                nc.sync.dma_start(out=out_words[:, cols], in_=y_mx[0][:, cols].bitcast(I32))
+        def store_codes(c0, c1):
+            nc.sync.dma_start(out=out_words[:, c0:c1], in_=y_mx[0][:, c0:c1].bitcast(I32))
 
         out_rows = out_0.rearrange("(p t) c -> p t c", t=LANES)
-        for t in range(LANES):
-            nc.vector.tensor_copy(out=windows[t][:].indirect(offsets[:]), in_=dense[t][:])
-            nc.sync.dma_start(out=out_rows[:, t, :], in_=windows[t][:])
-            if t < last_lane:
-                for k in range(len(CHUNKS)):
-                    round_lane(t, k)
+        for n, t in enumerate(ORDER):
+            nc.vector.tensor_copy(out=windows[n][:].indirect(offsets[:]), in_=dense[t][0][:])
+            nc.sync.dma_start(out=out_rows[:, t, :], in_=windows[n][:])
+            if n < LANES - 1:
+                place("scalar", n, 0, SPLIT)
+                pair(n)
+                place("gpsimd", n, SPLIT, direct)
 
-        for k in range(VECTOR_CHUNKS + 1):
-            round_lane(last_lane, k)
-        for k in range(VECTOR_CHUNKS + 1, len(CHUNKS)):
-            round_lane(last_lane, k)
-            weave(k - 1)
-        weave(len(CHUNKS) - 1)
-        weave(0)
-        for k in range(1, VECTOR_CHUNKS):
-            weave(k)
-            planes(k - 1)
-        for k in range(VECTOR_CHUNKS - 1, len(CHUNKS)):
-            planes(k)
-
-        out_scales = out_2.rearrange("a q c -> (a q) c").bitcast(I32)
+        last = LANES - 1
+        c0 = 0
+        for width in VECTOR_CHUNKS:
+            place("vector", last, c0, c0 + width)
+            c0 += width
+        pair(last)
+        chunks = [(direct, T)]
+        for k, width in enumerate(SCALAR_CHUNKS):
+            place("scalar", last, c0, c0 + width)
+            if k == 0:
+                nc.scalar.copy(out=y_bf[:, LANES * direct:].bitcast(U32).rearrange("p (c u) -> p c u", u=2),
+                               in_=paired[:].bitcast(U32).rearrange("p (u c) -> p c u", u=2))
+            chunks.append((sum(VECTOR_QUANT) if k == 0 else c0, c0 + width))
+            c0 += width
+        chunks[0], chunks[1] = chunks[1], chunks[0]
+        c0 = 0
+        for width in VECTOR_QUANT:
+            quantize(y_mx, y_bf, E4M3, c0, c0 + width)
+            c0 += width
+        store_codes(0, c0)
+        for k, (c0, c1) in enumerate(chunks):
+            quantize(y_mx, y_bf, E4M3, c0, c1)
+            if k == 1:
+                store_codes(c0, c1)
+            if k == len(chunks) - 2:
+                store_codes(chunks[0][0], c1)
+        store_codes(*chunks[-1])
         for q in range(P // 32):
             queue = nc.scalar if q % 2 == 0 else nc.sync
             queue.dma_start(out=out_scales[4 * q:4 * q + 4, :], in_=y_mx[1][32 * q:32 * q + 4, :].bitcast(I32))

@@ -27,7 +27,8 @@ PAIRED = 128
 VECTOR_QUANT = (512, 256, 128)
 
 DY_SCALAR = 192
-WG_VECTOR = 96
+WG_VECTOR = 40
+WG_LATE_VECTOR = 32
 WB_EARLY_VECTOR = 96
 WB_LATE_VECTOR = 64
 VECTOR_CHUNKS = (512, 448)
@@ -42,12 +43,12 @@ def tile_attend_gfilm_c_pl_kernel(tc, dy, x, wg, wb, offs, out_0, out_1, out_2):
         psum = ctx.enter_context(tc.psum_pool(name="psum", bufs=1))
 
         def load(src, name, c0, c1):
-            raw = sb.tile([P, LANES, c1 - c0], F32, name=name)
+            raw = sb.tile([P, LANES, c1 - c0], F32, name=name, align_bytes=64)
             nc.sync.dma_start(out=raw[:], in_=src.rearrange("(p j) c -> p j c", j=LANES)[:, :, c0:c1])
             return raw
 
         dy_raw = load(dy, "dy_raw", 0, N)
-        x_raw = [load(x, "x_raw%d" % h, h * N // 2, (h + 1) * N // 2) for h in range(2)]
+        x_raw = load(x, "x_raw", 0, N)
         wg_raw = load(wg, "wg_raw", 0, D)
         wb_raw = load(wb, "wb_raw", 0, D)
         offsets = sb.tile([P, N // 16], U16, name="offsets")
@@ -82,12 +83,13 @@ def tile_attend_gfilm_c_pl_kernel(tc, dy, x, wg, wb, offs, out_0, out_1, out_2):
         dg_mx = mx_tiles(N, "dg")
         nc.scalar.copy(out=woven(dy_bf[:, :LANES * DY_SCALAR]), in_=runs(dy_raw[:, :, :DY_SCALAR]))
         nc.vector.tensor_copy(out=woven(dy_bf[:, LANES * DY_SCALAR:]), in_=runs(dy_raw[:, :, DY_SCALAR:]))
-        for h in range(2):
-            cols = slice(h * N // 2, (h + 1) * N // 2)
-            nc.vector.tensor_tensor(out=woven(dg_bf[:, LANES * cols.start:LANES * cols.stop]),
-                                    in0=runs(dy_raw[:, :, cols]), in1=runs(x_raw[h][:]), op=mybir.AluOpType.mult)
         quantize(dy_mx, dy_bf, E5M2, 0, N)
-        quantize(dg_mx, dg_bf, E5M2, 0, N)
+        for c0 in range(0, N, N // 2):
+            cols = slice(c0, c0 + N // 2)
+            nc.vector.tensor_tensor(out=woven(dg_bf[:, LANES * c0:LANES * cols.stop]), in0=runs(dy_raw[:, :, cols]),
+                                    in1=runs(x_raw[:, :, cols]), op=mybir.AluOpType.mult)
+        for c0 in range(0, N, N // 2):
+            quantize(dg_mx, dg_bf, E5M2, c0, c0 + N // 2)
 
         w_bf = [sb.tile([P, D * LANES], BF16, name="w_bf%d" % s, align_bytes=64) for s in range(2)]
         w_mx = [mx_tiles(D, "w%d" % s) for s in range(2)]
@@ -97,24 +99,28 @@ def tile_attend_gfilm_c_pl_kernel(tc, dy, x, wg, wb, offs, out_0, out_1, out_2):
             src = raw[:].rearrange("p j (m t) -> p m j t", t=LANES)
             copy[engine](out=dealt[:, m0:m1, :, t0:t1], in_=src[:, m0:m1, :, t0:t1])
 
-        deal("scalar", wg_raw, 0, 0, LANES, WG_VECTOR, P)
-        deal("vector", wg_raw, 0, 0, LANES, 0, WG_VECTOR)
-        quantize(w_mx[0], w_bf[0], E4M3, 0, D // 2)
-        quantize(w_mx[0], w_bf[0], E4M3, D // 2, D)
+        deal("scalar", wg_raw, 0, 0, 2, WG_VECTOR, P)
+        deal("vector", wg_raw, 0, 0, 2, 0, WG_VECTOR)
+        deal("vector", wg_raw, 0, 2, LANES, 0, WG_LATE_VECTOR)
+        quantize(w_mx[0], w_bf[0], E4M3, 0, 2 * P)
+        deal("scalar", wg_raw, 0, 2, LANES, WG_LATE_VECTOR, P)
         for t0, m in ((0, WB_EARLY_VECTOR), (2, WB_LATE_VECTOR)):
             deal("vector", wb_raw, 1, t0, t0 + 2, 0, m)
             deal("scalar", wb_raw, 1, t0, t0 + 2, m, P)
             if t0 == 0:
                 quantize(w_mx[1], w_bf[1], E4M3, 0, P)
-        quantize(w_mx[1], w_bf[1], E4M3, P, 2 * P)
         quantize(w_mx[1], w_bf[1], E4M3, 2 * P, 4 * P)
+        wg_late = sb.tile([P, 2 * P], U32, name="wb_raw", align_bytes=64)
+        nc.vector.quantize_mx(out=wg_late[:].bitcast(E4M3), scales=w_mx[0][1][:, 2 * P:], in_=w_bf[0][:, LANES * 2 * P:])
+        quantize(w_mx[1], w_bf[1], E4M3, P, 2 * P)
 
         dense = {}
         for n, t in enumerate(ORDER):
             acc = psum.tile([P, N], F32, name="acc%d" % (n % 2))
             cols = slice(t * P, (t + 1) * P)
             for s, moving in enumerate((dg_mx, dy_mx)):
-                nc.tensor.matmul_mx(out=acc[:], lhsT=w_mx[s][0][:, cols].bitcast(E4M3), lhsT_scale=w_mx[s][1][:, cols],
+                codes = wg_late[:, (t - 2) * P:(t - 1) * P] if s == 0 and t >= 2 else w_mx[s][0][:, cols]
+                nc.tensor.matmul_mx(out=acc[:], lhsT=codes.bitcast(E4M3), lhsT_scale=w_mx[s][1][:, cols],
                                     rhs=moving[0][:].bitcast(E5M2), rhs_scale=moving[1][:],
                                     start=(s == 0), stop=(s == 1))
             parts = 1 if t == ORDER[0] else 1
@@ -126,7 +132,7 @@ def tile_attend_gfilm_c_pl_kernel(tc, dy, x, wg, wb, offs, out_0, out_1, out_2):
 
         y_bf = sb.tile([P, T * LANES], BF16, name="dy_codes", align_bytes=64)
         y_mx = mx_tiles(T, "y")
-        paired = sb.tile([P, LANES * PAIRED], BF16, name="dg_codes", align_bytes=64)
+        paired = sb.tile([P, LANES * PAIRED], BF16, name="w1_codes", align_bytes=64)
         direct = T - PAIRED
         copy["gpsimd"] = nc.gpsimd.tensor_copy
 

@@ -24,7 +24,7 @@ RUN = 4
 ORDER = (0, 2, 3, 1)
 SPLIT = 960
 PAIRED = 128
-VECTOR_QUANT = (512, 256, 128)
+QUANT = (((0, 256), (256, 512), (512, 768)), ((768, 1024), (1024, 1280), (1280, 1536)), ((1536, 1792), (1920, 2048), (1792, 1920)))
 
 DY_SCALAR = 192
 WG_VECTOR = 40
@@ -32,7 +32,7 @@ WG_LATE_VECTOR = 32
 WB_EARLY_VECTOR = 96
 WB_LATE_VECTOR = 64
 VECTOR_CHUNKS = (512, 448)
-SCALAR_CHUNKS = (192, 256, 256, 256)
+SCALAR_CHUNKS = (320, 256, 256, 128)
 
 
 def tile_attend_gfilm_c_pl_kernel(tc, dy, x, wg, wb, offs, out_0, out_1, out_2):
@@ -131,7 +131,14 @@ def tile_attend_gfilm_c_pl_kernel(tc, dy, x, wg, wb, offs, out_0, out_1, out_2):
                 dense[t].append(sums)
 
         y_bf = sb.tile([P, T * LANES], BF16, name="dy_codes", align_bytes=64)
-        y_mx = mx_tiles(T, "y")
+        y_codes = sb.tile([P, T], U32, name="y_codes", align_bytes=64)
+        y_scales = sb.tile([P, T // 4], U8, name="y_scales", align_bytes=64)
+
+        def quantize_y(c0, c1):
+            a, s0 = divmod(c0, T // 4)
+            nc.vector.quantize_mx(out=y_codes[:, c0:c1].bitcast(E4M3), scales=y_scales[4 * a:, s0:s0 + c1 - c0],
+                                  in_=y_bf[:, LANES * c0:LANES * c1])
+
         paired = sb.tile([P, LANES * PAIRED], BF16, name="w1_codes", align_bytes=64)
         direct = T - PAIRED
         copy["gpsimd"] = nc.gpsimd.tensor_copy
@@ -146,10 +153,10 @@ def tile_attend_gfilm_c_pl_kernel(tc, dy, x, wg, wb, offs, out_0, out_1, out_2):
             nc.scalar.copy(out=dst, in_=windows[n][:, direct:])
 
         out_words = out_1.rearrange("a p c l -> p (a c l)").bitcast(I32)
-        out_scales = out_2.rearrange("a q c -> (a q) c").bitcast(I32)
+        out_scales = out_2.bitcast(I32).rearrange("g (q b) (a c) -> (g q) a b c", b=4, a=4)
 
         def store_codes(c0, c1):
-            nc.sync.dma_start(out=out_words[:, c0:c1], in_=y_mx[0][:, c0:c1].bitcast(I32))
+            nc.sync.dma_start(out=out_words[:, c0:c1], in_=y_codes[:, c0:c1].bitcast(I32))
 
         out_rows = out_0.rearrange("(p t) c -> p t c", t=LANES)
         for n, t in enumerate(ORDER):
@@ -165,28 +172,18 @@ def tile_attend_gfilm_c_pl_kernel(tc, dy, x, wg, wb, offs, out_0, out_1, out_2):
         for width in VECTOR_CHUNKS:
             place("vector", last, c0, c0 + width)
             c0 += width
-        pair(last)
-        chunks = [(direct, T)]
         for k, width in enumerate(SCALAR_CHUNKS):
+            if k == len(SCALAR_CHUNKS) - 2:
+                pair(last)
             place("scalar", last, c0, c0 + width)
-            if k == 0:
+            if k == len(SCALAR_CHUNKS) - 2:
                 nc.scalar.copy(out=y_bf[:, LANES * direct:].bitcast(U32).rearrange("p (c u) -> p c u", u=2),
                                in_=paired[:].bitcast(U32).rearrange("p (u c) -> p c u", u=2))
-            chunks.append((sum(VECTOR_QUANT) if k == 0 else c0, c0 + width))
             c0 += width
-        chunks[0], chunks[1] = chunks[1], chunks[0]
-        c0 = 0
-        for width in VECTOR_QUANT:
-            quantize(y_mx, y_bf, E4M3, c0, c0 + width)
-            c0 += width
-        store_codes(0, c0)
-        for k, (c0, c1) in enumerate(chunks):
-            quantize(y_mx, y_bf, E4M3, c0, c1)
-            if k == 1:
-                store_codes(c0, c1)
-            if k == len(chunks) - 2:
-                store_codes(chunks[0][0], c1)
-        store_codes(*chunks[-1])
+        for group in QUANT:
+            for c0, c1 in group:
+                quantize_y(c0, c1)
+            store_codes(min(c[0] for c in group), max(c[1] for c in group))
         for q in range(P // 32):
             queue = nc.scalar if q % 2 == 0 else nc.sync
-            queue.dma_start(out=out_scales[4 * q:4 * q + 4, :], in_=y_mx[1][32 * q:32 * q + 4, :].bitcast(I32))
+            queue.dma_start(out=out_scales[q], in_=y_scales[32 * q:32 * q + 16, :].bitcast(I32))

@@ -22,17 +22,17 @@ P = 128
 LANES = 4
 RUN = 4
 ORDER = (0, 2, 3, 1)
-SPLIT = 960
-PAIRED = 128
-QUANT = (((0, 256), (256, 512), (512, 768)), ((768, 1024), (1024, 1280), (1280, 1536)), ((1536, 1792), (1920, 2048), (1792, 1920)))
+PAIRED = 256
+SPLIT = 1152
+QUANT = ((256, 256, 256), (256, 256, 256), (256, 128, 128))
 
 DY_SCALAR = 192
 WG_VECTOR = 40
 WG_LATE_VECTOR = 32
 WB_EARLY_VECTOR = 96
 WB_LATE_VECTOR = 64
-VECTOR_CHUNKS = (512, 448)
-SCALAR_CHUNKS = (320, 256, 256, 128)
+VECTOR_CHUNKS = (256, 384)
+SCALAR_CHUNKS = (384, 256, 256, 128, 128)
 
 
 def tile_attend_gfilm_c_pl_kernel(tc, dy, x, wg, wb, offs, out_0, out_1, out_2):
@@ -91,13 +91,14 @@ def tile_attend_gfilm_c_pl_kernel(tc, dy, x, wg, wb, offs, out_0, out_1, out_2):
         for c0 in range(0, N, N // 2):
             quantize(dg_mx, dg_bf, E5M2, c0, c0 + N // 2)
 
-        w_bf = [sb.tile([P, D * LANES], BF16, name="w_bf%d" % s, align_bytes=64) for s in range(2)]
-        w_mx = [mx_tiles(D, "w%d" % s) for s in range(2)]
+        w_bf = [sb.tile([P, D * LANES], BF16, name="w_bf%d" % u, align_bytes=64) for u in range(2)]
+        w_mx = [mx_tiles(D, "w%d" % u) for u in range(2)]
 
-        def deal(engine, raw, s, t0, t1, m0, m1):
-            dealt = w_bf[s][:].rearrange("p (t m j) -> p m j t", t=LANES, j=LANES)
+        def deal(engine, raw, s, t0, t1, m0, m1, j0=0):
+            u = t0 // 2
+            dealt = w_bf[u][:].rearrange("p (s e m j) -> p s m j e", s=2, e=2, j=LANES)
             src = raw[:].rearrange("p j (m t) -> p m j t", t=LANES)
-            copy[engine](out=dealt[:, m0:m1, :, t0:t1], in_=src[:, m0:m1, :, t0:t1])
+            copy[engine](out=dealt[:, s, m0:m1, j0:j0 + raw.shape[1], t0 - 2 * u:t1 - 2 * u], in_=src[:, m0:m1, :, t0:t1])
 
         deal("scalar", wg_raw, 0, 0, 2, WG_VECTOR, P)
         deal("vector", wg_raw, 0, 0, 2, 0, WG_VECTOR)
@@ -108,19 +109,17 @@ def tile_attend_gfilm_c_pl_kernel(tc, dy, x, wg, wb, offs, out_0, out_1, out_2):
             deal("vector", wb_raw, 1, t0, t0 + 2, 0, m)
             deal("scalar", wb_raw, 1, t0, t0 + 2, m, P)
             if t0 == 0:
-                quantize(w_mx[1], w_bf[1], E4M3, 0, P)
-        quantize(w_mx[1], w_bf[1], E4M3, 2 * P, 4 * P)
-        wg_late = sb.tile([P, 2 * P], U32, name="wb_raw", align_bytes=64)
-        nc.vector.quantize_mx(out=wg_late[:].bitcast(E4M3), scales=w_mx[0][1][:, 2 * P:], in_=w_bf[0][:, LANES * 2 * P:])
-        quantize(w_mx[1], w_bf[1], E4M3, P, 2 * P)
+                quantize(w_mx[0], w_bf[0], E4M3, 2 * P, 3 * P)
+        quantize(w_mx[0], w_bf[0], E4M3, 3 * P, 4 * P)
+        quantize(w_mx[1], w_bf[1], E4M3, 0, 4 * P)
 
         dense = {}
         for n, t in enumerate(ORDER):
             acc = psum.tile([P, N], F32, name="acc%d" % (n % 2))
-            cols = slice(t * P, (t + 1) * P)
             for s, moving in enumerate((dg_mx, dy_mx)):
-                codes = wg_late[:, (t - 2) * P:(t - 1) * P] if s == 0 and t >= 2 else w_mx[s][0][:, cols]
-                nc.tensor.matmul_mx(out=acc[:], lhsT=codes.bitcast(E4M3), lhsT_scale=w_mx[s][1][:, cols],
+                codes, scales = w_mx[t // 2]
+                cols = slice((2 * s + t % 2) * P, (2 * s + t % 2 + 1) * P)
+                nc.tensor.matmul_mx(out=acc[:], lhsT=codes[:, cols].bitcast(E4M3), lhsT_scale=scales[:, cols],
                                     rhs=moving[0][:].bitcast(E5M2), rhs_scale=moving[1][:],
                                     start=(s == 0), stop=(s == 1))
             parts = 1 if t == ORDER[0] else 1
@@ -139,18 +138,17 @@ def tile_attend_gfilm_c_pl_kernel(tc, dy, x, wg, wb, offs, out_0, out_1, out_2):
             nc.vector.quantize_mx(out=y_codes[:, c0:c1].bitcast(E4M3), scales=y_scales[4 * a:, s0:s0 + c1 - c0],
                                   in_=y_bf[:, LANES * c0:LANES * c1])
 
-        paired = sb.tile([P, LANES * PAIRED], BF16, name="w1_codes", align_bytes=64)
-        direct = T - PAIRED
+        paired = sb.tile([P, LANES * PAIRED], BF16, name="w0_codes", align_bytes=64)
         copy["gpsimd"] = nc.gpsimd.tensor_copy
 
         def place(engine, n, c0, c1):
             dst = y_bf[:, LANES * c0:LANES * c1].rearrange("p (c t) -> p t c", t=LANES)[:, ORDER[n], :]
             copy[engine](out=dst, in_=windows[n][:, c0:c1])
 
-        def pair(n):
+        def pair(engine, n):
             t = ORDER[n]
             dst = paired[:].rearrange("p (u c e) -> p u e c", u=2, e=2)[:, t // 2, t % 2, :]
-            nc.scalar.copy(out=dst, in_=windows[n][:, direct:])
+            copy[engine](out=dst, in_=windows[n][:, :PAIRED])
 
         out_words = out_1.rearrange("a p c l -> p (a c l)").bitcast(I32)
         out_scales = out_2.bitcast(I32).rearrange("g (q b) (a c) -> (g q) a b c", b=4, a=4)
@@ -163,27 +161,29 @@ def tile_attend_gfilm_c_pl_kernel(tc, dy, x, wg, wb, offs, out_0, out_1, out_2):
             nc.vector.tensor_copy(out=windows[n][:].indirect(offsets[:]), in_=dense[t][0][:])
             nc.sync.dma_start(out=out_rows[:, t, :], in_=windows[n][:])
             if n < LANES - 1:
-                place("scalar", n, 0, SPLIT)
-                pair(n)
-                place("gpsimd", n, SPLIT, direct)
+                pair("scalar", n)
+                place("scalar", n, PAIRED, SPLIT)
+                place("gpsimd", n, SPLIT, T)
 
         last = LANES - 1
-        c0 = 0
-        for width in VECTOR_CHUNKS:
+        pair("vector", last)
+        c0 = PAIRED
+        for k, width in enumerate(VECTOR_CHUNKS):
             place("vector", last, c0, c0 + width)
+            if k == 0:
+                nc.vector.tensor_copy(out=y_bf[:, :LANES * PAIRED].bitcast(I32).rearrange("p (c u) -> p c u", u=2),
+                                      in_=paired[:].bitcast(I32).rearrange("p (u c) -> p c u", u=2))
             c0 += width
-        for k, width in enumerate(SCALAR_CHUNKS):
-            if k == len(SCALAR_CHUNKS) - 2:
-                pair(last)
+        for width in SCALAR_CHUNKS:
             place("scalar", last, c0, c0 + width)
-            if k == len(SCALAR_CHUNKS) - 2:
-                nc.scalar.copy(out=y_bf[:, LANES * direct:].bitcast(U32).rearrange("p (c u) -> p c u", u=2),
-                               in_=paired[:].bitcast(U32).rearrange("p (u c) -> p c u", u=2))
             c0 += width
+        c0 = 0
         for group in QUANT:
-            for c0, c1 in group:
-                quantize_y(c0, c1)
-            store_codes(min(c[0] for c in group), max(c[1] for c in group))
+            first = c0
+            for width in group:
+                quantize_y(c0, c0 + width)
+                c0 += width
+            store_codes(first, c0)
         for q in range(P // 32):
             queue = nc.scalar if q % 2 == 0 else nc.sync
             queue.dma_start(out=out_scales[q], in_=y_scales[32 * q:32 * q + 16, :].bitcast(I32))

@@ -22,8 +22,9 @@ P = 128
 LANES = 4
 RUN = 4
 ORDER = (0, 2, 3, 1)
-PAIRED = 256
-SPLIT = 1152
+PAIRED = 512
+WEAVE = 256
+SPLIT = 1216
 QUANT = ((256, 256, 256), (256, 256, 256), (256, 128, 128))
 
 DY_SCALAR = 192
@@ -31,8 +32,8 @@ WG_VECTOR = 40
 WG_LATE_VECTOR = 32
 WB_EARLY_VECTOR = 96
 WB_LATE_VECTOR = 64
-VECTOR_CHUNKS = (256, 384)
-SCALAR_CHUNKS = (384, 256, 256, 128, 128)
+VECTOR_CHUNKS = (320,)
+SCALAR_CHUNKS = (448, 256, 256, 128, 128)
 
 
 def tile_attend_gfilm_c_pl_kernel(tc, dy, x, wg, wb, offs, out_0, out_1, out_2):
@@ -171,8 +172,10 @@ def tile_attend_gfilm_c_pl_kernel(tc, dy, x, wg, wb, offs, out_0, out_1, out_2):
         for k, width in enumerate(VECTOR_CHUNKS):
             place("vector", last, c0, c0 + width)
             if k == 0:
-                nc.vector.tensor_copy(out=y_bf[:, :LANES * PAIRED].bitcast(I32).rearrange("p (c u) -> p c u", u=2),
-                                      in_=paired[:].bitcast(I32).rearrange("p (u c) -> p c u", u=2))
+                for w0 in range(0, PAIRED, WEAVE):
+                    woven_words = y_bf[:, LANES * w0:LANES * (w0 + WEAVE)].bitcast(I32).rearrange("p (c u) -> p c u", u=2)
+                    nc.vector.tensor_copy(out=woven_words,
+                                          in_=paired[:].bitcast(I32).rearrange("p (u c) -> p c u", u=2)[:, w0:w0 + WEAVE])
             c0 += width
         for width in SCALAR_CHUNKS:
             place("scalar", last, c0, c0 + width)

@@ -22,9 +22,9 @@ P = 128
 LANES = 4
 RUN = 4
 ORDER = (0, 2, 3, 1)
-PAIRED = 512
-WEAVE = 256
-SPLIT = 1216
+PAIRED = 896
+WEAVE = 448
+SPLIT = 1280
 QUANT = ((256, 256, 256), (256, 256, 256), (256, 128, 128))
 
 DY_SCALAR = 192
@@ -32,8 +32,7 @@ WG_VECTOR = 40
 WG_LATE_VECTOR = 32
 WB_EARLY_VECTOR = 96
 WB_LATE_VECTOR = 64
-VECTOR_CHUNKS = (320,)
-SCALAR_CHUNKS = (448, 256, 256, 128, 128)
+SCALAR_CHUNKS = (384, 256, 256, 128, 128)
 
 
 def tile_attend_gfilm_c_pl_kernel(tc, dy, x, wg, wb, offs, out_0, out_1, out_2):
@@ -146,10 +145,10 @@ def tile_attend_gfilm_c_pl_kernel(tc, dy, x, wg, wb, offs, out_0, out_1, out_2):
             dst = y_bf[:, LANES * c0:LANES * c1].rearrange("p (c t) -> p t c", t=LANES)[:, ORDER[n], :]
             copy[engine](out=dst, in_=windows[n][:, c0:c1])
 
-        def pair(engine, n):
+        def pair(engine, n, c0, c1):
             t = ORDER[n]
-            dst = paired[:].rearrange("p (u c e) -> p u e c", u=2, e=2)[:, t // 2, t % 2, :]
-            copy[engine](out=dst, in_=windows[n][:, :PAIRED])
+            dst = paired[:].rearrange("p (u c e) -> p u e c", u=2, e=2)[:, t // 2, t % 2, c0:c1]
+            copy[engine](out=dst, in_=windows[n][:, c0:c1])
 
         out_words = out_1.rearrange("a p c l -> p (a c l)").bitcast(I32)
         out_scales = out_2.bitcast(I32).rearrange("g (q b) (a c) -> (g q) a b c", b=4, a=4)
@@ -162,21 +161,18 @@ def tile_attend_gfilm_c_pl_kernel(tc, dy, x, wg, wb, offs, out_0, out_1, out_2):
             nc.vector.tensor_copy(out=windows[n][:].indirect(offsets[:]), in_=dense[t][0][:])
             nc.sync.dma_start(out=out_rows[:, t, :], in_=windows[n][:])
             if n < LANES - 1:
-                pair("scalar", n)
+                pair("scalar", n, 0, PAIRED)
                 place("scalar", n, PAIRED, SPLIT)
                 place("gpsimd", n, SPLIT, T)
 
         last = LANES - 1
-        pair("vector", last)
+        for c0 in range(0, PAIRED, WEAVE):
+            pair("vector", last, c0, c0 + WEAVE)
+        pair_words = paired[:].bitcast(I32).rearrange("p (u c) -> p c u", u=2)
+        for c0 in range(0, PAIRED, WEAVE):
+            woven_words = y_bf[:, LANES * c0:LANES * (c0 + WEAVE)].bitcast(I32).rearrange("p (c u) -> p c u", u=2)
+            nc.vector.tensor_copy(out=woven_words, in_=pair_words[:, c0:c0 + WEAVE])
         c0 = PAIRED
-        for k, width in enumerate(VECTOR_CHUNKS):
-            place("vector", last, c0, c0 + width)
-            if k == 0:
-                for w0 in range(0, PAIRED, WEAVE):
-                    woven_words = y_bf[:, LANES * w0:LANES * (w0 + WEAVE)].bitcast(I32).rearrange("p (c u) -> p c u", u=2)
-                    nc.vector.tensor_copy(out=woven_words,
-                                          in_=paired[:].bitcast(I32).rearrange("p (u c) -> p c u", u=2)[:, w0:w0 + WEAVE])
-            c0 += width
         for width in SCALAR_CHUNKS:
             place("scalar", last, c0, c0 + width)
             c0 += width

@@ -22,16 +22,17 @@ P = 128
 LANES = 4
 RUN = 4
 ORDER = (0, 2, 3, 1)
-PAIRED = 896
-WEAVE = 448
-SPLIT = 1280
+PAIRED = 640
+WEAVE = 320
+SPLIT = 1216
 QUANT = ((256, 256, 256), (256, 256, 256), (256, 128, 128))
 
 DY_SCALAR = 192
 WG_VECTOR = 40
-WG_LATE_VECTOR = 32
-WB_EARLY_VECTOR = 96
+WG_LATE_VECTOR = 48
+WB_EARLY_VECTOR = 80
 WB_LATE_VECTOR = 64
+VECTOR_CHUNKS = (256,)
 SCALAR_CHUNKS = (384, 256, 256, 128, 128)
 
 
@@ -145,10 +146,10 @@ def tile_attend_gfilm_c_pl_kernel(tc, dy, x, wg, wb, offs, out_0, out_1, out_2):
             dst = y_bf[:, LANES * c0:LANES * c1].rearrange("p (c t) -> p t c", t=LANES)[:, ORDER[n], :]
             copy[engine](out=dst, in_=windows[n][:, c0:c1])
 
-        def pair(engine, n, c0, c1):
+        def pair(engine, n):
             t = ORDER[n]
-            dst = paired[:].rearrange("p (u c e) -> p u e c", u=2, e=2)[:, t // 2, t % 2, c0:c1]
-            copy[engine](out=dst, in_=windows[n][:, c0:c1])
+            dst = paired[:].rearrange("p (u c e) -> p u e c", u=2, e=2)[:, t // 2, t % 2, :]
+            copy[engine](out=dst, in_=windows[n][:, :PAIRED])
 
         out_words = out_1.rearrange("a p c l -> p (a c l)").bitcast(I32)
         out_scales = out_2.bitcast(I32).rearrange("g (q b) (a c) -> (g q) a b c", b=4, a=4)
@@ -161,18 +162,21 @@ def tile_attend_gfilm_c_pl_kernel(tc, dy, x, wg, wb, offs, out_0, out_1, out_2):
             nc.vector.tensor_copy(out=windows[n][:].indirect(offsets[:]), in_=dense[t][0][:])
             nc.sync.dma_start(out=out_rows[:, t, :], in_=windows[n][:])
             if n < LANES - 1:
-                pair("scalar", n, 0, PAIRED)
+                pair("scalar", n)
                 place("scalar", n, PAIRED, SPLIT)
                 place("gpsimd", n, SPLIT, T)
 
         last = LANES - 1
-        for c0 in range(0, PAIRED, WEAVE):
-            pair("vector", last, c0, c0 + WEAVE)
-        pair_words = paired[:].bitcast(I32).rearrange("p (u c) -> p c u", u=2)
-        for c0 in range(0, PAIRED, WEAVE):
-            woven_words = y_bf[:, LANES * c0:LANES * (c0 + WEAVE)].bitcast(I32).rearrange("p (c u) -> p c u", u=2)
-            nc.vector.tensor_copy(out=woven_words, in_=pair_words[:, c0:c0 + WEAVE])
+        pair("vector", last)
         c0 = PAIRED
+        for k, width in enumerate(VECTOR_CHUNKS):
+            place("vector", last, c0, c0 + width)
+            if k == 0:
+                for w0 in range(0, PAIRED, WEAVE):
+                    woven_words = y_bf[:, LANES * w0:LANES * (w0 + WEAVE)].bitcast(I32).rearrange("p (c u) -> p c u", u=2)
+                    nc.vector.tensor_copy(out=woven_words,
+                                          in_=paired[:].bitcast(I32).rearrange("p (u c) -> p c u", u=2)[:, w0:w0 + WEAVE])
+            c0 += width
         for width in SCALAR_CHUNKS:
             place("scalar", last, c0, c0 + width)
             c0 += width

@@ -21,19 +21,17 @@ E5M2 = mybir.dt.float8_e5m2_x4
 P = 128
 LANES = 4
 RUN = 4
-ORDER = (0, 2, 3, 1)
-PAIRED = 640
-WEAVE = 320
-SPLIT = 1216
-QUANT = ((256, 256, 256), (256, 256, 256), (256, 128, 128))
+HALF = N // 2
+EARLY = 896
+FILL = 256
+WEAVES = (("vector", 384), ("vector", 256), ("scalar", 256), ("scalar", 384), ("scalar", 256), ("scalar", 256), ("scalar", 256))
+QUANT = ((512,), (512, 256), (256, 256, 256))
 
 DY_SCALAR = 192
 WG_VECTOR = 40
 WG_LATE_VECTOR = 48
 WB_EARLY_VECTOR = 80
 WB_LATE_VECTOR = 64
-VECTOR_CHUNKS = (256,)
-SCALAR_CHUNKS = (384, 256, 256, 128, 128)
 
 
 def tile_attend_gfilm_c_pl_kernel(tc, dy, x, wg, wb, offs, out_0, out_1, out_2):
@@ -61,7 +59,6 @@ def tile_attend_gfilm_c_pl_kernel(tc, dy, x, wg, wb, offs, out_0, out_1, out_2):
             clear = nc.gpsimd if n == 2 else nc.vector
             clear.memset(window[:].bitcast(I32), 0)
             windows.append(window)
-        windows.append(windows[0])
 
         def runs(rows):
             return rows.rearrange("p j (c i) -> p c j i", i=RUN)
@@ -89,8 +86,7 @@ def tile_attend_gfilm_c_pl_kernel(tc, dy, x, wg, wb, offs, out_0, out_1, out_2):
             cols = slice(c0, c0 + N // 2)
             nc.vector.tensor_tensor(out=woven(dg_bf[:, LANES * c0:LANES * cols.stop]), in0=runs(dy_raw[:, :, cols]),
                                     in1=runs(x_raw[:, :, cols]), op=mybir.AluOpType.mult)
-        for c0 in range(0, N, N // 2):
-            quantize(dg_mx, dg_bf, E5M2, c0, c0 + N // 2)
+        quantize(dg_mx, dg_bf, E5M2, 0, HALF)
 
         w_bf = [sb.tile([P, D * LANES], BF16, name="w_bf%d" % u, align_bytes=64) for u in range(2)]
         w_mx = [mx_tiles(D, "w%d" % u) for u in range(2)]
@@ -103,90 +99,122 @@ def tile_attend_gfilm_c_pl_kernel(tc, dy, x, wg, wb, offs, out_0, out_1, out_2):
 
         deal("scalar", wg_raw, 0, 0, 2, WG_VECTOR, P)
         deal("vector", wg_raw, 0, 0, 2, 0, WG_VECTOR)
-        deal("vector", wg_raw, 0, 2, LANES, 0, WG_LATE_VECTOR)
+        quantize(dg_mx, dg_bf, E5M2, HALF, N)
         quantize(w_mx[0], w_bf[0], E4M3, 0, 2 * P)
+        deal("vector", wg_raw, 0, 2, LANES, 0, WG_LATE_VECTOR)
         deal("scalar", wg_raw, 0, 2, LANES, WG_LATE_VECTOR, P)
         for t0, m in ((0, WB_EARLY_VECTOR), (2, WB_LATE_VECTOR)):
             deal("vector", wb_raw, 1, t0, t0 + 2, 0, m)
             deal("scalar", wb_raw, 1, t0, t0 + 2, m, P)
             if t0 == 0:
                 quantize(w_mx[0], w_bf[0], E4M3, 2 * P, 3 * P)
-        quantize(w_mx[0], w_bf[0], E4M3, 3 * P, 4 * P)
+                quantize(w_mx[0], w_bf[0], E4M3, 3 * P, 4 * P)
         quantize(w_mx[1], w_bf[1], E4M3, 0, 4 * P)
 
-        dense = {}
-        for n, t in enumerate(ORDER):
-            acc = psum.tile([P, N], F32, name="acc%d" % (n % 2))
-            for s, moving in enumerate((dg_mx, dy_mx)):
-                codes, scales = w_mx[t // 2]
-                cols = slice((2 * s + t % 2) * P, (2 * s + t % 2 + 1) * P)
-                nc.tensor.matmul_mx(out=acc[:], lhsT=codes[:, cols].bitcast(E4M3), lhsT_scale=scales[:, cols],
-                                    rhs=moving[0][:].bitcast(E5M2), rhs_scale=moving[1][:],
-                                    start=(s == 0), stop=(s == 1))
-            parts = 1 if t == ORDER[0] else 1
-            dense[t] = []
-            for h in range(parts):
-                sums = sb.tile([P, N // parts], F32, name="sums%d_%d" % (t, h))
-                nc.scalar.copy(out=sums[:], in_=acc[:, h * N // parts:(h + 1) * N // parts])
-                dense[t].append(sums)
+        windows.append(sb.tile([P, T], F32, name="w_bf1", align_bytes=64))
+        nc.gpsimd.memset(windows[3][:].bitcast(I32), 0)
 
-        y_bf = sb.tile([P, T * LANES], BF16, name="dy_codes", align_bytes=64)
+        def product(out, t, s, samples):
+            codes, scales = w_mx[t // 2]
+            moving = (dg_mx, dy_mx)[s]
+            cols = slice((2 * s + t % 2) * P, (2 * s + t % 2 + 1) * P)
+            nc.tensor.matmul_mx(out=out, lhsT=codes[:, cols].bitcast(E4M3), lhsT_scale=scales[:, cols],
+                                rhs=moving[0][:, samples].bitcast(E5M2), rhs_scale=moving[1][:, samples],
+                                start=(s == 0), stop=(s == 1))
+
+        first, second, whole = slice(0, HALF), slice(HALF, N), slice(0, N)
+        banks = [psum.tile([P, N], F32, name="bank%d" % b) for b in range(6)]
+        early_groups = ((0, 0, first), (1, 1, first), (2, 1, second), (3, 0, second))
+        for s in range(2):
+            for b, t, samples in early_groups:
+                product(banks[b][:, first], t, s, samples)
+        for b, cols, t, samples in ((3, second, 2, first), (4, first, 2, second), (5, whole, 3, whole)):
+            for s in range(2):
+                product(banks[b][:, cols], t, s, samples)
+
+        out_rows = out_0.rearrange("(p t) c -> p t c", t=LANES)
+
+        def scatter_half(t, h, src):
+            nc.scalar.activation(out=windows[t][:].indirect(offsets[:, 16 * h:16 * (h + 1)]), in_=src,
+                                 func=mybir.ActivationFunctionType.Copy)
+
+        def store(t):
+            nc.sync.dma_start(out=out_rows[:, t, :], in_=windows[t][:])
+
+        sums0a = sb.tile([P, HALF], F32, name="sums0a")
+        nc.scalar.copy(out=sums0a[:], in_=banks[0][:, first])
+        sums1 = sb.tile([P, N], F32, name="sums1")
+        nc.vector.tensor_copy(out=sums1[:, first], in_=banks[1][:, first])
+        nc.vector.tensor_copy(out=sums1[:, second], in_=banks[2][:, first])
+        scatter_half(0, 0, sums0a[:])
+        nc.vector.tensor_copy(out=windows[1][:].indirect(offsets[:]), in_=sums1[:])
+        store(1)
+        sums02 = sb.tile([P, N], F32, name="sums02", align_bytes=64)
+        nc.scalar.copy(out=sums02[:], in_=banks[3][:])
+        sums2b = sb.tile([P, HALF], F32, name="sums2b")
+        nc.scalar.copy(out=sums2b[:], in_=banks[4][:, first])
+        sums3 = sb.tile([P, N], F32, name="sums3")
+        nc.scalar.copy(out=sums3[:], in_=banks[5][:])
+        scatter_half(0, 1, sums02[:, first])
+        store(0)
+        nc.vector.tensor_copy(out=windows[3][:].indirect(offsets[:]), in_=sums3[:])
+        store(3)
+        scatter_half(2, 0, sums02[:, second])
+
+        y_bf = sb.tile([P, T * LANES], BF16, name="y_bf", align_bytes=64)
         y_codes = sb.tile([P, T], U32, name="y_codes", align_bytes=64)
         y_scales = sb.tile([P, T // 4], U8, name="y_scales", align_bytes=64)
+        copy["gpsimd"] = nc.gpsimd.tensor_copy
 
         def quantize_y(c0, c1):
             a, s0 = divmod(c0, T // 4)
             nc.vector.quantize_mx(out=y_codes[:, c0:c1].bitcast(E4M3), scales=y_scales[4 * a:, s0:s0 + c1 - c0],
                                   in_=y_bf[:, LANES * c0:LANES * c1])
 
-        paired = sb.tile([P, LANES * PAIRED], BF16, name="w0_codes", align_bytes=64)
-        copy["gpsimd"] = nc.gpsimd.tensor_copy
+        early = sb.tile([P, LANES * EARLY], BF16, name="early", align_bytes=64)
+        late = sb.tile([P, LANES * (T - EARLY)], BF16, name="sums02", align_bytes=64)
 
-        def place(engine, n, c0, c1):
-            dst = y_bf[:, LANES * c0:LANES * c1].rearrange("p (c t) -> p t c", t=LANES)[:, ORDER[n], :]
-            copy[engine](out=dst, in_=windows[n][:, c0:c1])
+        def pair_early(engine, t):
+            dst = early[:].rearrange("p (u c e) -> p u e c", u=2, e=2)[:, t // 2, t % 2, :]
+            copy[engine](out=dst, in_=windows[t][:, :EARLY])
 
-        def pair(engine, n):
-            t = ORDER[n]
-            dst = paired[:].rearrange("p (u c e) -> p u e c", u=2, e=2)[:, t // 2, t % 2, :]
-            copy[engine](out=dst, in_=windows[n][:, :PAIRED])
+        def pair_late(engine, t, c0, c1):
+            dst = late[:].rearrange("p (u c e) -> p u e c", u=2, e=2)[:, t // 2, t % 2, c0 - EARLY:c1 - EARLY]
+            copy[engine](out=dst, in_=windows[t][:, c0:c1])
+
+        def weave(engine, c0, c1):
+            word = I32 if engine == "vector" else U32
+            pairs, base = (early, 0) if c0 < EARLY else (late, EARLY)
+            src = pairs[:].bitcast(word).rearrange("p (u c) -> p c u", u=2)[:, c0 - base:c1 - base]
+            dst = y_bf[:, LANES * c0:LANES * c1].bitcast(word).rearrange("p (c u) -> p c u", u=2)
+            copy[engine](out=dst, in_=src)
+
+        pair_late("scalar", 1, EARLY, EARLY + FILL)
+        scatter_half(2, 1, sums2b[:])
+        store(2)
+        for t in (1, 0):
+            pair_early("gpsimd", t)
+        pair_late("scalar", 1, EARLY + FILL, T)
+        pair_late("scalar", 0, EARLY, T)
+        for t in (3, 2):
+            pair_early("vector", t)
+            pair_late("vector", t, EARLY, T)
 
         out_words = out_1.rearrange("a p c l -> p (a c l)").bitcast(I32)
         out_scales = out_2.bitcast(I32).rearrange("g (q b) (a c) -> (g q) a b c", b=4, a=4)
-
-        def store_codes(c0, c1):
-            nc.sync.dma_start(out=out_words[:, c0:c1], in_=y_codes[:, c0:c1].bitcast(I32))
-
-        out_rows = out_0.rearrange("(p t) c -> p t c", t=LANES)
-        for n, t in enumerate(ORDER):
-            nc.vector.tensor_copy(out=windows[n][:].indirect(offsets[:]), in_=dense[t][0][:])
-            nc.sync.dma_start(out=out_rows[:, t, :], in_=windows[n][:])
-            if n < LANES - 1:
-                pair("scalar", n)
-                place("scalar", n, PAIRED, SPLIT)
-                place("gpsimd", n, SPLIT, T)
-
-        last = LANES - 1
-        pair("vector", last)
-        c0 = PAIRED
-        for k, width in enumerate(VECTOR_CHUNKS):
-            place("vector", last, c0, c0 + width)
-            if k == 0:
-                for w0 in range(0, PAIRED, WEAVE):
-                    woven_words = y_bf[:, LANES * w0:LANES * (w0 + WEAVE)].bitcast(I32).rearrange("p (c u) -> p c u", u=2)
-                    nc.vector.tensor_copy(out=woven_words,
-                                          in_=paired[:].bitcast(I32).rearrange("p (u c) -> p c u", u=2)[:, w0:w0 + WEAVE])
-            c0 += width
-        for width in SCALAR_CHUNKS:
-            place("scalar", last, c0, c0 + width)
-            c0 += width
+        weaves = list(WEAVES)
+        woven_to = 0
         c0 = 0
         for group in QUANT:
-            first = c0
+            start = c0
             for width in group:
+                while woven_to < min(T, c0 + width + 128):
+                    engine, step = weaves.pop(0)
+                    weave(engine, woven_to, woven_to + step)
+                    woven_to += step
                 quantize_y(c0, c0 + width)
                 c0 += width
-            store_codes(first, c0)
+            nc.sync.dma_start(out=out_words[:, start:c0], in_=y_codes[:, start:c0].bitcast(I32))
         for q in range(P // 32):
             queue = nc.scalar if q % 2 == 0 else nc.sync
             queue.dma_start(out=out_scales[q], in_=y_scales[32 * q:32 * q + 16, :].bitcast(I32))

@@ -24,8 +24,9 @@ RUN = 4
 HALF = N // 2
 EARLY = 896
 FILL = 256
-WEAVES = (("vector", 384), ("vector", 256), ("scalar", 256), ("scalar", 384), ("scalar", 256), ("scalar", 256), ("scalar", 256))
-QUANT = ((512,), (512, 256), (256, 256, 256))
+AHEAD = 384
+WEAVES = (("vector", 512), ("vector", 384), ("vector", 256), ("scalar", 256), ("scalar", 256), ("scalar", 256), ("scalar", 128))
+QUANT = ((256, 256, 256), (256, 256), (256, 256), (256,))
 
 DY_SCALAR = 192
 WG_VECTOR = 40
@@ -107,8 +108,8 @@ def tile_attend_gfilm_c_pl_kernel(tc, dy, x, wg, wb, offs, out_0, out_1, out_2):
             deal("vector", wb_raw, 1, t0, t0 + 2, 0, m)
             deal("scalar", wb_raw, 1, t0, t0 + 2, m, P)
             if t0 == 0:
-                quantize(w_mx[0], w_bf[0], E4M3, 2 * P, 3 * P)
                 quantize(w_mx[0], w_bf[0], E4M3, 3 * P, 4 * P)
+                quantize(w_mx[0], w_bf[0], E4M3, 2 * P, 3 * P)
         quantize(w_mx[1], w_bf[1], E4M3, 0, 4 * P)
 
         windows.append(sb.tile([P, T], F32, name="w_bf1", align_bytes=64))
@@ -124,11 +125,11 @@ def tile_attend_gfilm_c_pl_kernel(tc, dy, x, wg, wb, offs, out_0, out_1, out_2):
 
         first, second, whole = slice(0, HALF), slice(HALF, N), slice(0, N)
         banks = [psum.tile([P, N], F32, name="bank%d" % b) for b in range(6)]
-        early_groups = ((0, 0, first), (1, 1, first), (2, 1, second), (3, 0, second))
+        early_groups = ((1, 1, first), (0, 0, first), (2, 1, second), (3, 0, second))
         for s in range(2):
             for b, t, samples in early_groups:
                 product(banks[b][:, first], t, s, samples)
-        for b, cols, t, samples in ((3, second, 2, first), (4, first, 2, second), (5, whole, 3, whole)):
+        for b, cols, t, samples in ((5, whole, 3, whole), (3, second, 2, first), (4, first, 2, second)):
             for s in range(2):
                 product(banks[b][:, cols], t, s, samples)
 
@@ -141,20 +142,20 @@ def tile_attend_gfilm_c_pl_kernel(tc, dy, x, wg, wb, offs, out_0, out_1, out_2):
         def store(t):
             nc.sync.dma_start(out=out_rows[:, t, :], in_=windows[t][:])
 
+        sums1 = sb.tile([P, N], F32, name="sums1")
+        nc.scalar.copy(out=sums1[:, first], in_=banks[1][:, first])
         sums0a = sb.tile([P, HALF], F32, name="sums0a")
         nc.scalar.copy(out=sums0a[:], in_=banks[0][:, first])
-        sums1 = sb.tile([P, N], F32, name="sums1")
-        nc.vector.tensor_copy(out=sums1[:, first], in_=banks[1][:, first])
         nc.vector.tensor_copy(out=sums1[:, second], in_=banks[2][:, first])
         scatter_half(0, 0, sums0a[:])
         nc.vector.tensor_copy(out=windows[1][:].indirect(offsets[:]), in_=sums1[:])
         store(1)
+        sums3 = sb.tile([P, N], F32, name="sums3")
+        nc.scalar.copy(out=sums3[:], in_=banks[5][:])
         sums02 = sb.tile([P, N], F32, name="sums02", align_bytes=64)
         nc.scalar.copy(out=sums02[:], in_=banks[3][:])
         sums2b = sb.tile([P, HALF], F32, name="sums2b")
         nc.scalar.copy(out=sums2b[:], in_=banks[4][:, first])
-        sums3 = sb.tile([P, N], F32, name="sums3")
-        nc.scalar.copy(out=sums3[:], in_=banks[5][:])
         scatter_half(0, 1, sums02[:, first])
         store(0)
         nc.vector.tensor_copy(out=windows[3][:].indirect(offsets[:]), in_=sums3[:])
@@ -174,31 +175,32 @@ def tile_attend_gfilm_c_pl_kernel(tc, dy, x, wg, wb, offs, out_0, out_1, out_2):
         early = sb.tile([P, LANES * EARLY], BF16, name="early", align_bytes=64)
         late = sb.tile([P, LANES * (T - EARLY)], BF16, name="sums02", align_bytes=64)
 
-        def pair_early(engine, t):
-            dst = early[:].rearrange("p (u c e) -> p u e c", u=2, e=2)[:, t // 2, t % 2, :]
-            copy[engine](out=dst, in_=windows[t][:, :EARLY])
+        mid = EARLY + FILL
+        stretches = ((0, EARLY, early[:]), (EARLY, mid, late[:, :LANES * FILL]), (mid, T, late[:, LANES * FILL:]))
 
-        def pair_late(engine, t, c0, c1):
-            dst = late[:].rearrange("p (u c e) -> p u e c", u=2, e=2)[:, t // 2, t % 2, c0 - EARLY:c1 - EARLY]
+        def pair(engine, t, stretch):
+            c0, c1, pairs = stretches[stretch]
+            dst = pairs.rearrange("p (u c e) -> p u e c", u=2, e=2)[:, t // 2, t % 2, :]
             copy[engine](out=dst, in_=windows[t][:, c0:c1])
 
         def weave(engine, c0, c1):
             word = I32 if engine == "vector" else U32
-            pairs, base = (early, 0) if c0 < EARLY else (late, EARLY)
-            src = pairs[:].bitcast(word).rearrange("p (u c) -> p c u", u=2)[:, c0 - base:c1 - base]
+            base, end, pairs = [s for s in stretches if s[0] <= c0 < s[1]][0]
+            src = pairs.bitcast(word).rearrange("p (u c) -> p c u", u=2)[:, c0 - base:c1 - base]
             dst = y_bf[:, LANES * c0:LANES * c1].bitcast(word).rearrange("p (c u) -> p c u", u=2)
             copy[engine](out=dst, in_=src)
 
-        pair_late("scalar", 1, EARLY, EARLY + FILL)
+        pair("scalar", 1, 1)
         scatter_half(2, 1, sums2b[:])
         store(2)
         for t in (1, 0):
-            pair_early("gpsimd", t)
-        pair_late("scalar", 1, EARLY + FILL, T)
-        pair_late("scalar", 0, EARLY, T)
+            pair("gpsimd", t, 0)
+        pair("scalar", 0, 1)
+        for t in (1, 0):
+            pair("scalar", t, 2)
         for t in (3, 2):
-            pair_early("vector", t)
-            pair_late("vector", t, EARLY, T)
+            for stretch in range(3):
+                pair("vector", t, stretch)
 
         out_words = out_1.rearrange("a p c l -> p (a c l)").bitcast(I32)
         out_scales = out_2.bitcast(I32).rearrange("g (q b) (a c) -> (g q) a b c", b=4, a=4)
@@ -208,7 +210,7 @@ def tile_attend_gfilm_c_pl_kernel(tc, dy, x, wg, wb, offs, out_0, out_1, out_2):
         for group in QUANT:
             start = c0
             for width in group:
-                while woven_to < min(T, c0 + width + 128):
+                while woven_to < min(T, c0 + width + AHEAD):
                     engine, step = weaves.pop(0)
                     weave(engine, woven_to, woven_to + step)
                     woven_to += step

@@ -22,10 +22,11 @@ P = 128
 LANES = 4
 RUN = 4
 HALF = N // 2
-EARLY = 896
-FILL = 256
-AHEAD = 384
-WEAVES = (("vector", 512), ("vector", 384), ("vector", 256), ("scalar", 256), ("scalar", 256), ("scalar", 256), ("scalar", 128))
+EARLY = 832
+MID = 256
+FILL = 192
+AHEAD = 320
+WEAVES = (("vector", 512), ("vector", 320), ("scalar", 256), ("vector", 128), ("scalar", 320), ("scalar", 256), ("scalar", 256))
 QUANT = ((256, 256, 256), (256, 256), (256, 256), (256,))
 
 DY_SCALAR = 192
@@ -125,7 +126,7 @@ def tile_attend_gfilm_c_pl_kernel(tc, dy, x, wg, wb, offs, out_0, out_1, out_2):
 
         first, second, whole = slice(0, HALF), slice(HALF, N), slice(0, N)
         banks = [psum.tile([P, N], F32, name="bank%d" % b) for b in range(6)]
-        early_groups = ((1, 1, first), (0, 0, first), (2, 1, second), (3, 0, second))
+        early_groups = ((1, 1, first), (2, 1, second), (0, 0, first), (3, 0, second))
         for s in range(2):
             for b, t, samples in early_groups:
                 product(banks[b][:, first], t, s, samples)
@@ -144,9 +145,9 @@ def tile_attend_gfilm_c_pl_kernel(tc, dy, x, wg, wb, offs, out_0, out_1, out_2):
 
         sums1 = sb.tile([P, N], F32, name="sums1")
         nc.scalar.copy(out=sums1[:, first], in_=banks[1][:, first])
+        nc.scalar.copy(out=sums1[:, second], in_=banks[2][:, first])
         sums0a = sb.tile([P, HALF], F32, name="sums0a")
         nc.scalar.copy(out=sums0a[:], in_=banks[0][:, first])
-        nc.vector.tensor_copy(out=sums1[:, second], in_=banks[2][:, first])
         scatter_half(0, 0, sums0a[:])
         nc.vector.tensor_copy(out=windows[1][:].indirect(offsets[:]), in_=sums1[:])
         store(1)
@@ -175,13 +176,13 @@ def tile_attend_gfilm_c_pl_kernel(tc, dy, x, wg, wb, offs, out_0, out_1, out_2):
         early = sb.tile([P, LANES * EARLY], BF16, name="early", align_bytes=64)
         late = sb.tile([P, LANES * (T - EARLY)], BF16, name="sums02", align_bytes=64)
 
-        mid = EARLY + FILL
-        stretches = ((0, EARLY, early[:]), (EARLY, mid, late[:, :LANES * FILL]), (mid, T, late[:, LANES * FILL:]))
+        mid = EARLY + MID
+        stretches = ((0, EARLY, early[:]), (EARLY, mid, late[:, :LANES * MID]), (mid, T, late[:, LANES * MID:]))
 
-        def pair(engine, t, stretch):
+        def pair(engine, t, stretch, cols=slice(None)):
             c0, c1, pairs = stretches[stretch]
-            dst = pairs.rearrange("p (u c e) -> p u e c", u=2, e=2)[:, t // 2, t % 2, :]
-            copy[engine](out=dst, in_=windows[t][:, c0:c1])
+            dst = pairs.rearrange("p (u c e) -> p u e c", u=2, e=2)[:, t // 2, t % 2, cols]
+            copy[engine](out=dst, in_=windows[t][:, c0:c1][:, cols])
 
         def weave(engine, c0, c1):
             word = I32 if engine == "vector" else U32
@@ -190,17 +191,19 @@ def tile_attend_gfilm_c_pl_kernel(tc, dy, x, wg, wb, offs, out_0, out_1, out_2):
             dst = y_bf[:, LANES * c0:LANES * c1].bitcast(word).rearrange("p (c u) -> p c u", u=2)
             copy[engine](out=dst, in_=src)
 
-        pair("scalar", 1, 1)
+        pair("scalar", 1, 2, slice(0, FILL))
         scatter_half(2, 1, sums2b[:])
         store(2)
         for t in (1, 0):
             pair("gpsimd", t, 0)
-        pair("scalar", 0, 1)
+        pair("scalar", 0, 2)
+        pair("scalar", 1, 2, slice(FILL, None))
+        for stretch in range(3):
+            pair("vector", 3, stretch)
         for t in (1, 0):
-            pair("scalar", t, 2)
-        for t in (3, 2):
-            for stretch in range(3):
-                pair("vector", t, stretch)
+            pair("vector", t, 1)
+        for stretch in range(3):
+            pair("vector", 2, stretch)
 
         out_words = out_1.rearrange("a p c l -> p (a c l)").bitcast(I32)
         out_scales = out_2.bitcast(I32).rearrange("g (q b) (a c) -> (g q) a b c", b=4, a=4)

@@ -22,18 +22,16 @@ P = 128
 LANES = 4
 RUN = 4
 HALF = N // 2
-EARLY = 832
-MID = 256
+EARLY = 1216
 FILL = 192
-AHEAD = 320
-WEAVES = (("vector", 512), ("vector", 320), ("scalar", 256), ("vector", 128), ("scalar", 320), ("scalar", 256), ("scalar", 256))
-QUANT = ((256, 256, 256), (256, 256), (256, 256), (256,))
+AHEAD = 256
+WEAVES = (("vector", 256), ("scalar", 256), ("vector", 192), ("scalar", 256), ("scalar", 256), ("scalar", 320), ("scalar", 256), ("scalar", 256))
+QUANT = ((256, 256, 256), (256, 256, 256), (256, 256))
 
 DY_SCALAR = 192
-WG_VECTOR = 40
-WG_LATE_VECTOR = 48
-WB_EARLY_VECTOR = 80
-WB_LATE_VECTOR = 64
+WB_VECTOR = 80
+WG_EARLY_VECTOR = 80
+WG_LATE_VECTOR = 32
 
 
 def tile_attend_gfilm_c_pl_kernel(tc, dy, x, wg, wb, offs, out_0, out_1, out_2):
@@ -49,11 +47,12 @@ def tile_attend_gfilm_c_pl_kernel(tc, dy, x, wg, wb, offs, out_0, out_1, out_2):
             return raw
 
         dy_raw = load(dy, "dy_raw", 0, N)
-        x_raw = load(x, "x_raw", 0, N)
-        wg_raw = load(wg, "wg_raw", 0, D)
+        x_first = load(x, "x_first", 0, HALF)
         wb_raw = load(wb, "wb_raw", 0, D)
         offsets = sb.tile([P, N // 16], U16, name="offsets")
         nc.sync.dma_start(offsets[:], offs)
+        wg_raw = load(wg, "wg_raw", 0, D)
+        x_second = load(x, "x_second", HALF, N)
 
         windows = []
         for n in range(3):
@@ -78,90 +77,107 @@ def tile_attend_gfilm_c_pl_kernel(tc, dy, x, wg, wb, offs, out_0, out_1, out_2):
                                   in_=values[:, LANES * c0:LANES * c1])
 
         dy_bf = sb.tile([P, N * LANES], BF16, name="dy_bf", align_bytes=64)
-        dg_bf = sb.tile([P, N * LANES], BF16, name="dg_bf", align_bytes=64)
+        dg_bf = [sb.tile([P, HALF * LANES], BF16, name="dg_bf%d" % h, align_bytes=64) for h in range(2)]
         dy_mx = mx_tiles(N, "dy")
         dg_mx = mx_tiles(N, "dg")
+        first, second, whole = slice(0, HALF), slice(HALF, N), slice(0, N)
         nc.scalar.copy(out=woven(dy_bf[:, :LANES * DY_SCALAR]), in_=runs(dy_raw[:, :, :DY_SCALAR]))
         nc.vector.tensor_copy(out=woven(dy_bf[:, LANES * DY_SCALAR:]), in_=runs(dy_raw[:, :, DY_SCALAR:]))
+
+        def multiply(h, x_raw, samples):
+            nc.vector.tensor_tensor(out=woven(dg_bf[h][:]), in0=runs(dy_raw[:, :, samples]), in1=runs(x_raw[:]),
+                                    op=mybir.AluOpType.mult)
+
+        def quantize_dg(h, samples):
+            nc.vector.quantize_mx(out=dg_mx[0][:, samples].bitcast(E5M2), scales=dg_mx[1][:, samples], in_=dg_bf[h][:])
+
+        multiply(0, x_first, first)
         quantize(dy_mx, dy_bf, E5M2, 0, N)
-        for c0 in range(0, N, N // 2):
-            cols = slice(c0, c0 + N // 2)
-            nc.vector.tensor_tensor(out=woven(dg_bf[:, LANES * c0:LANES * cols.stop]), in0=runs(dy_raw[:, :, cols]),
-                                    in1=runs(x_raw[:, :, cols]), op=mybir.AluOpType.mult)
-        quantize(dg_mx, dg_bf, E5M2, 0, HALF)
+        quantize_dg(0, first)
 
         w_bf = [sb.tile([P, D * LANES], BF16, name="w_bf%d" % u, align_bytes=64) for u in range(2)]
         w_mx = [mx_tiles(D, "w%d" % u) for u in range(2)]
 
-        def deal(engine, raw, s, t0, t1, m0, m1, j0=0):
+        def deal(engine, raw, s, t0, t1, m0, m1):
             u = t0 // 2
             dealt = w_bf[u][:].rearrange("p (s e m j) -> p s m j e", s=2, e=2, j=LANES)
             src = raw[:].rearrange("p j (m t) -> p m j t", t=LANES)
-            copy[engine](out=dealt[:, s, m0:m1, j0:j0 + raw.shape[1], t0 - 2 * u:t1 - 2 * u], in_=src[:, m0:m1, :, t0:t1])
+            copy[engine](out=dealt[:, s, m0:m1, :, t0 - 2 * u:t1 - 2 * u], in_=src[:, m0:m1, :, t0:t1])
 
-        deal("scalar", wg_raw, 0, 0, 2, WG_VECTOR, P)
-        deal("vector", wg_raw, 0, 0, 2, 0, WG_VECTOR)
-        quantize(dg_mx, dg_bf, E5M2, HALF, N)
-        quantize(w_mx[0], w_bf[0], E4M3, 0, 2 * P)
-        deal("vector", wg_raw, 0, 2, LANES, 0, WG_LATE_VECTOR)
-        deal("scalar", wg_raw, 0, 2, LANES, WG_LATE_VECTOR, P)
-        for t0, m in ((0, WB_EARLY_VECTOR), (2, WB_LATE_VECTOR)):
-            deal("vector", wb_raw, 1, t0, t0 + 2, 0, m)
-            deal("scalar", wb_raw, 1, t0, t0 + 2, m, P)
+        for t0 in (0, 2):
+            deal("vector", wb_raw, 0, t0, t0 + 2, 0, WB_VECTOR)
+            deal("scalar", wb_raw, 0, t0, t0 + 2, WB_VECTOR, P)
+        for u in range(2):
+            quantize(w_mx[u], w_bf[u], E4M3, 0, 2 * P)
+        for t0, m in ((0, WG_EARLY_VECTOR), (2, WG_LATE_VECTOR)):
+            deal("vector", wg_raw, 1, t0, t0 + 2, 0, m)
+            deal("scalar", wg_raw, 1, t0, t0 + 2, m, P)
             if t0 == 0:
-                quantize(w_mx[0], w_bf[0], E4M3, 3 * P, 4 * P)
                 quantize(w_mx[0], w_bf[0], E4M3, 2 * P, 3 * P)
-        quantize(w_mx[1], w_bf[1], E4M3, 0, 4 * P)
-
-        windows.append(sb.tile([P, T], F32, name="w_bf1", align_bytes=64))
-        nc.gpsimd.memset(windows[3][:].bitcast(I32), 0)
+                quantize(w_mx[0], w_bf[0], E4M3, 3 * P, 4 * P)
+        quantize(w_mx[1], w_bf[1], E4M3, 2 * P, 4 * P)
 
         def product(out, t, s, samples):
             codes, scales = w_mx[t // 2]
-            moving = (dg_mx, dy_mx)[s]
+            moving = (dy_mx, dg_mx)[s]
             cols = slice((2 * s + t % 2) * P, (2 * s + t % 2 + 1) * P)
             nc.tensor.matmul_mx(out=out, lhsT=codes[:, cols].bitcast(E4M3), lhsT_scale=scales[:, cols],
                                 rhs=moving[0][:, samples].bitcast(E5M2), rhs_scale=moving[1][:, samples],
                                 start=(s == 0), stop=(s == 1))
 
-        first, second, whole = slice(0, HALF), slice(HALF, N), slice(0, N)
         banks = [psum.tile([P, N], F32, name="bank%d" % b) for b in range(6)]
-        early_groups = ((1, 1, first), (2, 1, second), (0, 0, first), (3, 0, second))
-        for s in range(2):
-            for b, t, samples in early_groups:
-                product(banks[b][:, first], t, s, samples)
-        for b, cols, t, samples in ((5, whole, 3, whole), (3, second, 2, first), (4, first, 2, second)):
-            for s in range(2):
-                product(banks[b][:, cols], t, s, samples)
+        for t in range(2):
+            product(banks[2 * t][:, first], t, 0, first)
+        for t in range(2):
+            product(banks[2 * t + 1][:, first], t, 0, second)
+        for t in (3, 2):
+            product(banks[2 + t][:], t, 0, whole)
+        for t in range(2):
+            product(banks[2 * t][:, first], t, 1, first)
 
         out_rows = out_0.rearrange("(p t) c -> p t c", t=LANES)
 
-        def scatter_half(t, h, src):
-            nc.scalar.activation(out=windows[t][:].indirect(offsets[:, 16 * h:16 * (h + 1)]), in_=src,
-                                 func=mybir.ActivationFunctionType.Copy)
+        def scatter_half(engine, t, h, src):
+            window = windows[t][:].indirect(offsets[:, 16 * h:16 * (h + 1)])
+            if engine == "scalar":
+                nc.scalar.activation(out=window, in_=src, func=mybir.ActivationFunctionType.Copy)
+            else:
+                nc.vector.tensor_copy(out=window, in_=src)
 
         def store(t):
             nc.sync.dma_start(out=out_rows[:, t, :], in_=windows[t][:])
 
-        sums1 = sb.tile([P, N], F32, name="sums1")
-        nc.scalar.copy(out=sums1[:, first], in_=banks[1][:, first])
-        nc.scalar.copy(out=sums1[:, second], in_=banks[2][:, first])
         sums0a = sb.tile([P, HALF], F32, name="sums0a")
         nc.scalar.copy(out=sums0a[:], in_=banks[0][:, first])
-        scatter_half(0, 0, sums0a[:])
-        nc.vector.tensor_copy(out=windows[1][:].indirect(offsets[:]), in_=sums1[:])
-        store(1)
-        sums3 = sb.tile([P, N], F32, name="sums3")
-        nc.scalar.copy(out=sums3[:], in_=banks[5][:])
-        sums02 = sb.tile([P, N], F32, name="sums02", align_bytes=64)
-        nc.scalar.copy(out=sums02[:], in_=banks[3][:])
-        sums2b = sb.tile([P, HALF], F32, name="sums2b")
-        nc.scalar.copy(out=sums2b[:], in_=banks[4][:, first])
-        scatter_half(0, 1, sums02[:, first])
+        scatter_half("scalar", 0, 0, sums0a[:])
+        multiply(1, x_second, second)
+        sums1a = sb.tile([P, HALF], F32, name="x_second", align_bytes=64)
+        nc.vector.tensor_copy(out=sums1a[:], in_=banks[2][:, first])
+        quantize_dg(1, second)
+        windows.append(sb.tile([P, T], F32, name="dg_bf1", align_bytes=64))
+        nc.gpsimd.memset(windows[3][:].bitcast(I32), 0)
+        scatter_half("vector", 1, 0, sums1a[:])
+        for t in range(2):
+            product(banks[2 * t + 1][:, first], t, 1, second)
+        for t in (3, 2):
+            product(banks[2 + t][:], t, 1, whole)
+        sums0b = sb.tile([P, HALF], F32, name="sums0b")
+        nc.scalar.copy(out=sums0b[:], in_=banks[1][:, first])
+        sums1b = sb.tile([P, HALF], F32, name="sums1b")
+        nc.scalar.copy(out=sums1b[:], in_=banks[3][:, first])
+        scatter_half("scalar", 0, 1, sums0b[:])
         store(0)
+        sums3 = sb.tile([P, N], F32, name="sums3")
+        nc.vector.tensor_copy(out=sums3[:], in_=banks[5][:])
+        scatter_half("vector", 1, 1, sums1b[:])
+        store(1)
         nc.vector.tensor_copy(out=windows[3][:].indirect(offsets[:]), in_=sums3[:])
         store(3)
-        scatter_half(2, 0, sums02[:, second])
+        sums2a = sb.tile([P, HALF], F32, name="sums2a", align_bytes=64)
+        nc.scalar.copy(out=sums2a[:], in_=banks[4][:, first])
+        sums2b = sb.tile([P, HALF], F32, name="sums2b")
+        nc.scalar.copy(out=sums2b[:], in_=banks[4][:, second])
+        scatter_half("scalar", 2, 0, sums2a[:])
 
         y_bf = sb.tile([P, T * LANES], BF16, name="y_bf", align_bytes=64)
         y_codes = sb.tile([P, T], U32, name="y_codes", align_bytes=64)
@@ -174,10 +190,9 @@ def tile_attend_gfilm_c_pl_kernel(tc, dy, x, wg, wb, offs, out_0, out_1, out_2):
                                   in_=y_bf[:, LANES * c0:LANES * c1])
 
         early = sb.tile([P, LANES * EARLY], BF16, name="early", align_bytes=64)
-        late = sb.tile([P, LANES * (T - EARLY)], BF16, name="sums02", align_bytes=64)
+        late = sb.tile([P, LANES * (T - EARLY)], BF16, name="sums2a", align_bytes=64)
 
-        mid = EARLY + MID
-        stretches = ((0, EARLY, early[:]), (EARLY, mid, late[:, :LANES * MID]), (mid, T, late[:, LANES * MID:]))
+        stretches = ((0, EARLY, early[:]), (EARLY, T, late[:]))
 
         def pair(engine, t, stretch, cols=slice(None)):
             c0, c1, pairs = stretches[stretch]
@@ -191,19 +206,16 @@ def tile_attend_gfilm_c_pl_kernel(tc, dy, x, wg, wb, offs, out_0, out_1, out_2):
             dst = y_bf[:, LANES * c0:LANES * c1].bitcast(word).rearrange("p (c u) -> p c u", u=2)
             copy[engine](out=dst, in_=src)
 
-        pair("scalar", 1, 2, slice(0, FILL))
-        scatter_half(2, 1, sums2b[:])
+        pair("scalar", 0, 1, slice(0, FILL))
+        scatter_half("scalar", 2, 1, sums2b[:])
         store(2)
-        for t in (1, 0):
+        for t in range(2):
             pair("gpsimd", t, 0)
-        pair("scalar", 0, 2)
-        pair("scalar", 1, 2, slice(FILL, None))
-        for stretch in range(3):
-            pair("vector", 3, stretch)
-        for t in (1, 0):
-            pair("vector", t, 1)
-        for stretch in range(3):
-            pair("vector", 2, stretch)
+        pair("scalar", 1, 1)
+        pair("scalar", 0, 1, slice(FILL, None))
+        for stretch in range(2):
+            for t in (3, 2):
+                pair("vector", t, stretch)
 
         out_words = out_1.rearrange("a p c l -> p (a c l)").bitcast(I32)
         out_scales = out_2.bitcast(I32).rearrange("g (q b) (a c) -> (g q) a b c", b=4, a=4)

@@ -117,23 +117,23 @@ def tile_attend_gfilm_c_pl_kernel(tc, dy, x, wg, wb, offs, out_0, out_1, out_2):
                 quantize(w_mx[0], w_bf[0], E4M3, 3 * P, 4 * P)
         quantize(w_mx[1], w_bf[1], E4M3, 2 * P, 4 * P)
 
-        def product(out, t, s, samples):
+        def product(out, t, s, samples, closes=True):
             codes, scales = w_mx[t // 2]
             moving = (dy_mx, dg_mx)[s]
             cols = slice((2 * s + t % 2) * P, (2 * s + t % 2 + 1) * P)
             nc.tensor.matmul_mx(out=out, lhsT=codes[:, cols].bitcast(E4M3), lhsT_scale=scales[:, cols],
                                 rhs=moving[0][:, samples].bitcast(E5M2), rhs_scale=moving[1][:, samples],
-                                start=(s == 0), stop=(s == 1))
+                                start=(s == 0), stop=(s == 1 and closes))
 
-        banks = [psum.tile([P, N], F32, name="bank%d" % b) for b in range(6)]
+        banks = {b: psum.tile([P, N], F32, name="bank%d" % b) for b in (0, 1, 2, 3, 5)}
         for t in range(2):
             product(banks[2 * t][:, first], t, 0, first)
         for t in range(2):
             product(banks[2 * t + 1][:, first], t, 0, second)
-        for t in (3, 2):
-            product(banks[2 + t][:], t, 0, whole)
+        product(banks[5][:], 3, 0, whole)
         for t in range(2):
             product(banks[2 * t][:, first], t, 1, first)
+        product(banks[5][:, first], 3, 1, first, closes=False)
 
         out_rows = out_0.rearrange("(p t) c -> p t c", t=LANES)
 
@@ -149,6 +149,9 @@ def tile_attend_gfilm_c_pl_kernel(tc, dy, x, wg, wb, offs, out_0, out_1, out_2):
 
         sums0a = sb.tile([P, HALF], F32, name="sums0a")
         nc.scalar.copy(out=sums0a[:], in_=banks[0][:, first])
+        banks[4] = psum.tile([P, N], F32, name="bank0")
+        product(banks[4][:], 2, 0, whole)
+        product(banks[4][:, first], 2, 1, first, closes=False)
         scatter_half("scalar", 0, 0, sums0a[:])
         multiply(1, x_second, second)
         sums1a = sb.tile([P, HALF], F32, name="x_second", align_bytes=64)
@@ -160,7 +163,7 @@ def tile_attend_gfilm_c_pl_kernel(tc, dy, x, wg, wb, offs, out_0, out_1, out_2):
         for t in range(2):
             product(banks[2 * t + 1][:, first], t, 1, second)
         for t in (3, 2):
-            product(banks[2 + t][:], t, 1, whole)
+            product(banks[2 + t][:, second], t, 1, second)
         sums0b = sb.tile([P, HALF], F32, name="sums0b")
         nc.scalar.copy(out=sums0b[:], in_=banks[1][:, first])
         sums1b = sb.tile([P, HALF], F32, name="sums1b")

@@ -49,10 +49,10 @@ def tile_attend_gfilm_c_pl_kernel(tc, dy, x, wg, wb, offs, out_0, out_1, out_2):
         dy_raw = load(dy, "dy_raw", 0, N)
         x_first = load(x, "x_first", 0, HALF)
         wb_raw = load(wb, "wb_raw", 0, D)
-        offsets = sb.tile([P, N // 16], U16, name="offsets")
-        nc.sync.dma_start(offsets[:], offs)
         wg_raw = load(wg, "wg_raw", 0, D)
         x_second = load(x, "x_second", HALF, N)
+        offsets = sb.tile([P, N // 16], U16, name="offsets")
+        nc.sync.dma_start(offsets[:], offs)
 
         windows = []
         for n in range(3):

@@ -28,8 +28,8 @@ AHEAD = 256
 WEAVES = (("vector", 256), ("scalar", 256), ("vector", 192), ("scalar", 256), ("scalar", 256), ("scalar", 320), ("scalar", 256), ("scalar", 256))
 QUANT = ((256, 256, 256), (256, 256, 256), (256, 256))
 
-DY_SCALAR = 192
-WB_VECTOR = 80
+DY_SCALAR = 256
+WB_VECTOR = 56
 WG_EARLY_VECTOR = 80
 WG_LATE_VECTOR = 32
 
@@ -41,13 +41,13 @@ def tile_attend_gfilm_c_pl_kernel(tc, dy, x, wg, wb, offs, out_0, out_1, out_2):
         sb = ctx.enter_context(tc.tile_pool(name="sb", bufs=1))
         psum = ctx.enter_context(tc.psum_pool(name="psum", bufs=1))
 
-        def load(src, name, c0, c1):
+        def load(src, name, c0, c1, queue=nc.sync):
             raw = sb.tile([P, LANES, c1 - c0], F32, name=name, align_bytes=64)
-            nc.sync.dma_start(out=raw[:], in_=src.rearrange("(p j) c -> p j c", j=LANES)[:, :, c0:c1])
+            queue.dma_start(out=raw[:], in_=src.rearrange("(p j) c -> p j c", j=LANES)[:, :, c0:c1])
             return raw
 
         dy_raw = load(dy, "dy_raw", 0, N)
-        x_first = load(x, "x_first", 0, HALF)
+        x_first = load(x, "x_first", 0, HALF, nc.scalar)
         wb_raw = load(wb, "wb_raw", 0, D)
         wg_raw = load(wg, "wg_raw", 0, D)
         x_second = load(x, "x_second", HALF, N)

@@ -1,6 +1,7 @@
 from contextlib import ExitStack
 
 import concourse.mybir as mybir
+from concourse.masks import make_identity
 
 F = 512
 D = 512
@@ -22,11 +23,11 @@ P = 128
 LANES = 4
 RUN = 4
 HALF = N // 2
-EARLY = 1216
-FILL = 192
-AHEAD = 256
-WEAVES = (("vector", 256), ("scalar", 256), ("vector", 192), ("scalar", 256), ("scalar", 256), ("scalar", 320), ("scalar", 256), ("scalar", 256))
-QUANT = ((256, 256, 256), (256, 256, 256), (256, 256))
+CHUNK = 256
+PAIRED = 1280
+GPSIMD = 1216
+SCALAR_WEAVE = 160
+STORES = (768, 1536, 2048)
 
 DY_SCALAR = 256
 WB_VECTOR = 56
@@ -60,6 +61,9 @@ def tile_attend_gfilm_c_pl_kernel(tc, dy, x, wg, wb, offs, out_0, out_1, out_2):
             clear = nc.gpsimd if n == 2 else nc.vector
             clear.memset(window[:].bitcast(I32), 0)
             windows.append(window)
+
+        identity = sb.tile([P, P], F32, name="identity")
+        make_identity(nc, identity[:])
 
         def runs(rows):
             return rows.rearrange("p j (c i) -> p c j i", i=RUN)
@@ -182,59 +186,87 @@ def tile_attend_gfilm_c_pl_kernel(tc, dy, x, wg, wb, offs, out_0, out_1, out_2):
         nc.scalar.copy(out=sums2b[:], in_=banks[4][:, second])
         scatter_half("scalar", 2, 0, sums2a[:])
 
-        y_bf = sb.tile([P, T * LANES], BF16, name="y_bf", align_bytes=64)
         y_codes = sb.tile([P, T], U32, name="y_codes", align_bytes=64)
         y_scales = sb.tile([P, T // 4], U8, name="y_scales", align_bytes=64)
+        y_bf = [sb.tile([P, CHUNK * LANES], BF16, name="y_bf%d" % k, align_bytes=64) for k in range(T // CHUNK)]
         copy["gpsimd"] = nc.gpsimd.tensor_copy
+        out_words = out_1.rearrange("a p c l -> p (a c l)").bitcast(I32)
 
-        def quantize_y(c0, c1):
+        def quantize_y(k):
+            c0, c1 = k * CHUNK, (k + 1) * CHUNK
             a, s0 = divmod(c0, T // 4)
-            nc.vector.quantize_mx(out=y_codes[:, c0:c1].bitcast(E4M3), scales=y_scales[4 * a:, s0:s0 + c1 - c0],
-                                  in_=y_bf[:, LANES * c0:LANES * c1])
+            nc.vector.quantize_mx(out=y_codes[:, c0:c1].bitcast(E4M3), scales=y_scales[4 * a:, s0:s0 + CHUNK],
+                                  in_=y_bf[k][:])
+            if c1 in STORES:
+                start = ((0,) + STORES)[STORES.index(c1)]
+                nc.sync.dma_start(out=out_words[:, start:c1], in_=y_codes[:, start:c1].bitcast(I32))
 
-        early = sb.tile([P, LANES * EARLY], BF16, name="early", align_bytes=64)
-        late = sb.tile([P, LANES * (T - EARLY)], BF16, name="sums2a", align_bytes=64)
+        pairs = sb.tile([P, LANES * PAIRED], BF16, name="pairs", align_bytes=64)
 
-        stretches = ((0, EARLY, early[:]), (EARLY, T, late[:]))
+        def pair(engine, t, c0, c1):
+            dst = pairs[:].rearrange("p (u c e) -> p u e c", u=2, e=2)[:, t // 2, t % 2, c0:c1]
+            copy[engine](out=dst, in_=windows[t][:, c0:c1])
 
-        def pair(engine, t, stretch, cols=slice(None)):
-            c0, c1, pairs = stretches[stretch]
-            dst = pairs.rearrange("p (u c e) -> p u e c", u=2, e=2)[:, t // 2, t % 2, cols]
-            copy[engine](out=dst, in_=windows[t][:, c0:c1][:, cols])
-
-        def weave(engine, c0, c1):
+        def weave(engine, k, c0=0, c1=CHUNK):
             word = I32 if engine == "vector" else U32
-            base, end, pairs = [s for s in stretches if s[0] <= c0 < s[1]][0]
-            src = pairs.bitcast(word).rearrange("p (u c) -> p c u", u=2)[:, c0 - base:c1 - base]
-            dst = y_bf[:, LANES * c0:LANES * c1].bitcast(word).rearrange("p (c u) -> p c u", u=2)
-            copy[engine](out=dst, in_=src)
+            src = pairs[:].bitcast(word).rearrange("p (u c) -> p c u", u=2)[:, k * CHUNK + c0:k * CHUNK + c1]
+            copy[engine](out=y_bf[k][:].bitcast(word).rearrange("p (c u) -> p c u", u=2)[:, c0:c1], in_=src)
 
-        pair("scalar", 0, 1, slice(0, FILL))
+        turned_chunks = range(PAIRED // CHUNK, T // CHUNK)
+        spare = {0: ("bank4", "bank6", "bank7"), 1: ("bank1", "bank2", "bank3"), 2: ("bank5", "bank0", "bank4")}
+        across, staged, back = {}, {}, {}
+
+        def turn_lane(t):
+            for i, k in enumerate(turned_chunks):
+                if (t // 2, k) not in across:
+                    across[t // 2, k] = psum.tile([P, 2, 2, P], F32, name=spare[t // 2][i])
+                for b in range(2):
+                    c0 = k * CHUNK + b * P
+                    nc.tensor.transpose(across[t // 2, k][:, b, t % 2, :], windows[t][:, c0:c0 + P], identity[:])
+
+        def round_pairs(u, k):
+            staged[u, k] = sb.tile([P, 2, 2 * P], BF16, name="staged%d_%d" % (u, k), align_bytes=64)
+            nc.scalar.copy(out=staged[u, k][:].rearrange("c b (p e) -> c b p e", e=2),
+                           in_=across[u, k][:].rearrange("c b e p -> c b p e"))
+
+        def turn_back(u, k):
+            if k not in back:
+                back[k] = psum.tile([P, 2, 2, P], F32, name=spare[2][k - turned_chunks[0]])
+            for b in range(2):
+                nc.tensor.transpose(back[k][:, b, u, :], staged[u, k][:, b, :].bitcast(F32), identity[:])
+
+        def place(k):
+            nc.scalar.copy(out=y_bf[k][:].bitcast(F32).rearrange("p (b c u) -> p b c u", b=2, u=2),
+                           in_=back[k][:].rearrange("p b u c -> p b c u"))
+
+        for t in range(2):
+            pair("scalar", t, GPSIMD, PAIRED)
         scatter_half("scalar", 2, 1, sums2b[:])
         store(2)
         for t in range(2):
-            pair("gpsimd", t, 0)
-        pair("scalar", 1, 1)
-        pair("scalar", 0, 1, slice(FILL, None))
-        for stretch in range(2):
-            for t in (3, 2):
-                pair("vector", t, stretch)
+            pair("gpsimd", t, 0, GPSIMD)
+        for t in (0, 1, 3, 2):
+            turn_lane(t)
+        pair("vector", 3, 0, PAIRED)
+        pair("vector", 2, 0, PAIRED // 2)
+        pair("vector", 2, PAIRED // 2, PAIRED)
+        for k in turned_chunks:
+            round_pairs(0, k)
+            turn_back(0, k)
+        first_turned = turned_chunks[0]
+        for k in turned_chunks:
+            round_pairs(1, k)
+            turn_back(1, k)
+        weave("scalar", first_turned - 1, CHUNK - SCALAR_WEAVE, CHUNK)
+        for k in turned_chunks:
+            place(k)
+        weave("vector", 0)
+        for k in range(T // CHUNK):
+            if k + 1 < first_turned:
+                weave("vector", k + 1, 0, CHUNK - SCALAR_WEAVE if k + 2 == first_turned else CHUNK)
+            quantize_y(k)
 
-        out_words = out_1.rearrange("a p c l -> p (a c l)").bitcast(I32)
         out_scales = out_2.bitcast(I32).rearrange("g (q b) (a c) -> (g q) a b c", b=4, a=4)
-        weaves = list(WEAVES)
-        woven_to = 0
-        c0 = 0
-        for group in QUANT:
-            start = c0
-            for width in group:
-                while woven_to < min(T, c0 + width + AHEAD):
-                    engine, step = weaves.pop(0)
-                    weave(engine, woven_to, woven_to + step)
-                    woven_to += step
-                quantize_y(c0, c0 + width)
-                c0 += width
-            nc.sync.dma_start(out=out_words[:, start:c0], in_=y_codes[:, start:c0].bitcast(I32))
         for q in range(P // 32):
             queue = nc.scalar if q % 2 == 0 else nc.sync
             queue.dma_start(out=out_scales[q], in_=y_scales[32 * q:32 * q + 16, :].bitcast(I32))

@@ -26,7 +26,7 @@ HALF = N // 2
 CHUNK = 256
 PAIRED = 1280
 GPSIMD = 1216
-SCALAR_WEAVE = 160
+SCALAR_WEAVE = 256
 STORES = (768, 1536, 2048)
 
 DY_SCALAR = 256
@@ -55,15 +55,15 @@ def tile_attend_gfilm_c_pl_kernel(tc, dy, x, wg, wb, offs, out_0, out_1, out_2):
         offsets = sb.tile([P, N // 16], U16, name="offsets")
         nc.sync.dma_start(offsets[:], offs)
 
+        identity = sb.tile([P, P], F32, name="identity")
+        make_identity(nc, identity[:])
+
         windows = []
         for n in range(3):
             window = sb.tile([P, T], F32, name="window%d" % n)
             clear = nc.gpsimd if n == 2 else nc.vector
             clear.memset(window[:].bitcast(I32), 0)
             windows.append(window)
-
-        identity = sb.tile([P, P], F32, name="identity")
-        make_identity(nc, identity[:])
 
         def runs(rows):
             return rows.rearrange("p j (c i) -> p c j i", i=RUN)
@@ -213,21 +213,21 @@ def tile_attend_gfilm_c_pl_kernel(tc, dy, x, wg, wb, offs, out_0, out_1, out_2):
             copy[engine](out=y_bf[k][:].bitcast(word).rearrange("p (c u) -> p c u", u=2)[:, c0:c1], in_=src)
 
         turned_chunks = range(PAIRED // CHUNK, T // CHUNK)
-        spare = {0: ("bank4", "bank6", "bank7"), 1: ("bank1", "bank2", "bank3"), 2: ("bank5", "bank0", "bank4")}
+        spare = {0: ("bank4", "bank6", "bank7"), 1: ("bank1", "bank4", "bank6"), 2: ("bank1", "bank4", "bank6")}
         across, staged, back = {}, {}, {}
 
-        def turn_lane(t):
-            for i, k in enumerate(turned_chunks):
-                if (t // 2, k) not in across:
-                    across[t // 2, k] = psum.tile([P, 2, 2, P], F32, name=spare[t // 2][i])
-                for b in range(2):
-                    c0 = k * CHUNK + b * P
-                    nc.tensor.transpose(across[t // 2, k][:, b, t % 2, :], windows[t][:, c0:c0 + P], identity[:])
+        def turn_lane(t, k):
+            if (t // 2, k) not in across:
+                across[t // 2, k] = psum.tile([P, 2, 2, P], F32, name=spare[t // 2][k - turned_chunks[0]])
+            for b in range(2):
+                c0 = k * CHUNK + b * P
+                nc.tensor.transpose(across[t // 2, k][:, b, t % 2, :], windows[t][:, c0:c0 + P], identity[:])
 
-        def round_pairs(u, k):
-            staged[u, k] = sb.tile([P, 2, 2 * P], BF16, name="staged%d_%d" % (u, k), align_bytes=64)
-            nc.scalar.copy(out=staged[u, k][:].rearrange("c b (p e) -> c b p e", e=2),
-                           in_=across[u, k][:].rearrange("c b e p -> c b p e"))
+        def round_pairs(u, k, engine="scalar", blocks=slice(0, 2)):
+            if (u, k) not in staged:
+                staged[u, k] = sb.tile([P, 2, 2 * P], BF16, name="staged%d_%d" % (u, k), align_bytes=64)
+            copy[engine](out=staged[u, k][:].rearrange("c b (p e) -> c b p e", e=2)[:, blocks],
+                         in_=across[u, k][:].rearrange("c b e p -> c b p e")[:, blocks])
 
         def turn_back(u, k):
             if k not in back:
@@ -245,25 +245,28 @@ def tile_attend_gfilm_c_pl_kernel(tc, dy, x, wg, wb, offs, out_0, out_1, out_2):
         store(2)
         for t in range(2):
             pair("gpsimd", t, 0, GPSIMD)
-        for t in (0, 1, 3, 2):
-            turn_lane(t)
+        for t in range(2):
+            for k in turned_chunks:
+                turn_lane(t, k)
         pair("vector", 3, 0, PAIRED)
         pair("vector", 2, 0, PAIRED // 2)
         pair("vector", 2, PAIRED // 2, PAIRED)
         for k in turned_chunks:
+            turn_lane(3, k)
+            turn_lane(2, k)
             round_pairs(0, k)
-            turn_back(0, k)
         first_turned = turned_chunks[0]
         for k in turned_chunks:
             round_pairs(1, k)
+            turn_back(0, k)
             turn_back(1, k)
         weave("scalar", first_turned - 1, CHUNK - SCALAR_WEAVE, CHUNK)
         for k in turned_chunks:
             place(k)
         weave("vector", 0)
         for k in range(T // CHUNK):
-            if k + 1 < first_turned:
-                weave("vector", k + 1, 0, CHUNK - SCALAR_WEAVE if k + 2 == first_turned else CHUNK)
+            if k + 2 < first_turned:
+                weave("vector", k + 1)
             quantize_y(k)
 
         out_scales = out_2.bitcast(I32).rearrange("g (q b) (a c) -> (g q) a b c", b=4, a=4)

@@ -24,9 +24,7 @@ LANES = 4
 RUN = 4
 HALF = N // 2
 CHUNK = 256
-PAIRED = 1280
-GPSIMD = 1216
-SCALAR_WEAVE = 256
+PAIRED = 1152
 STORES = (768, 1536, 2048)
 
 DY_SCALAR = 256
@@ -192,11 +190,11 @@ def tile_attend_gfilm_c_pl_kernel(tc, dy, x, wg, wb, offs, out_0, out_1, out_2):
         copy["gpsimd"] = nc.gpsimd.tensor_copy
         out_words = out_1.rearrange("a p c l -> p (a c l)").bitcast(I32)
 
-        def quantize_y(k):
-            c0, c1 = k * CHUNK, (k + 1) * CHUNK
+        def quantize_y(c0, c1):
             a, s0 = divmod(c0, T // 4)
-            nc.vector.quantize_mx(out=y_codes[:, c0:c1].bitcast(E4M3), scales=y_scales[4 * a:, s0:s0 + CHUNK],
-                                  in_=y_bf[k][:])
+            k, first_col = divmod(c0, CHUNK)
+            nc.vector.quantize_mx(out=y_codes[:, c0:c1].bitcast(E4M3), scales=y_scales[4 * a:, s0:s0 + c1 - c0],
+                                  in_=y_bf[k][:, LANES * first_col:LANES * (first_col + c1 - c0)])
             if c1 in STORES:
                 start = ((0,) + STORES)[STORES.index(c1)]
                 nc.sync.dma_start(out=out_words[:, start:c1], in_=y_codes[:, start:c1].bitcast(I32))
@@ -212,62 +210,70 @@ def tile_attend_gfilm_c_pl_kernel(tc, dy, x, wg, wb, offs, out_0, out_1, out_2):
             src = pairs[:].bitcast(word).rearrange("p (u c) -> p c u", u=2)[:, k * CHUNK + c0:k * CHUNK + c1]
             copy[engine](out=y_bf[k][:].bitcast(word).rearrange("p (c u) -> p c u", u=2)[:, c0:c1], in_=src)
 
-        turned_chunks = range(PAIRED // CHUNK, T // CHUNK)
-        spare = {0: ("bank4", "bank6", "bank7"), 1: ("bank1", "bank4", "bank6"), 2: ("bank1", "bank4", "bank6")}
+        units = ((PAIRED, 1), (1280, 2), (1536, 2), (1792, 2))
+        first_banks = ("bank4", "bank6", "bank7", "bank2")
+        later_banks = ("bank1", "bank4", "bank6", "bank7")
         across, staged, back = {}, {}, {}
 
-        def turn_lane(t, k):
-            if (t // 2, k) not in across:
-                across[t // 2, k] = psum.tile([P, 2, 2, P], F32, name=spare[t // 2][k - turned_chunks[0]])
-            for b in range(2):
-                c0 = k * CHUNK + b * P
-                nc.tensor.transpose(across[t // 2, k][:, b, t % 2, :], windows[t][:, c0:c0 + P], identity[:])
+        def turn_lane(t, n):
+            c0, blocks = units[n]
+            if (t // 2, n) not in across:
+                across[t // 2, n] = psum.tile([P, blocks, 2, P], F32, name=(first_banks, later_banks)[t // 2][n])
+            for b in range(blocks):
+                nc.tensor.transpose(across[t // 2, n][:, b, t % 2, :], windows[t][:, c0 + b * P:c0 + (b + 1) * P],
+                                    identity[:])
 
-        def round_pairs(u, k, engine="scalar", blocks=slice(0, 2)):
-            if (u, k) not in staged:
-                staged[u, k] = sb.tile([P, 2, 2 * P], BF16, name="staged%d_%d" % (u, k), align_bytes=64)
-            copy[engine](out=staged[u, k][:].rearrange("c b (p e) -> c b p e", e=2)[:, blocks],
-                         in_=across[u, k][:].rearrange("c b e p -> c b p e")[:, blocks])
+        def round_pairs(u, n):
+            staged[u, n] = sb.tile([P, units[n][1], 2 * P], BF16, name="staged%d_%d" % (u, n), align_bytes=64)
+            nc.scalar.copy(out=staged[u, n][:].rearrange("c b (p e) -> c b p e", e=2),
+                           in_=across[u, n][:].rearrange("c b e p -> c b p e"))
 
-        def turn_back(u, k):
-            if k not in back:
-                back[k] = psum.tile([P, 2, 2, P], F32, name=spare[2][k - turned_chunks[0]])
-            for b in range(2):
-                nc.tensor.transpose(back[k][:, b, u, :], staged[u, k][:, b, :].bitcast(F32), identity[:])
+        def turn_back(n):
+            back[n] = psum.tile([P, units[n][1], 2, P], F32, name=later_banks[n])
+            for u in range(2):
+                for b in range(units[n][1]):
+                    nc.tensor.transpose(back[n][:, b, u, :], staged[u, n][:, b, :].bitcast(F32), identity[:])
 
-        def place(k):
-            nc.scalar.copy(out=y_bf[k][:].bitcast(F32).rearrange("p (b c u) -> p b c u", b=2, u=2),
-                           in_=back[k][:].rearrange("p b u c -> p b c u"))
+        def place(n, b0, b1):
+            c0 = units[n][0]
+            values = y_bf[c0 // CHUNK][:, LANES * (c0 % CHUNK):]
+            nc.scalar.copy(out=values.bitcast(F32).rearrange("p (b c u) -> p b c u", c=P, u=2)[:, b0:b1],
+                           in_=back[n][:].rearrange("p b u c -> p b c u")[:, b0:b1])
 
         for t in range(2):
-            pair("scalar", t, GPSIMD, PAIRED)
+            turn_lane(t, 0)
+        round_pairs(0, 0)
         scatter_half("scalar", 2, 1, sums2b[:])
         store(2)
         for t in range(2):
-            pair("gpsimd", t, 0, GPSIMD)
+            pair("gpsimd", t, 0, PAIRED)
         for t in range(2):
-            for k in turned_chunks:
-                turn_lane(t, k)
+            for n in range(1, len(units)):
+                turn_lane(t, n)
         pair("vector", 3, 0, PAIRED)
         pair("vector", 2, 0, PAIRED // 2)
         pair("vector", 2, PAIRED // 2, PAIRED)
-        for k in turned_chunks:
-            turn_lane(3, k)
-            turn_lane(2, k)
-            round_pairs(0, k)
-        first_turned = turned_chunks[0]
-        for k in turned_chunks:
-            round_pairs(1, k)
-            turn_back(0, k)
-            turn_back(1, k)
-        weave("scalar", first_turned - 1, CHUNK - SCALAR_WEAVE, CHUNK)
-        for k in turned_chunks:
-            place(k)
+        for n in range(len(units)):
+            turn_lane(3, n)
+            turn_lane(2, n)
+            if n:
+                round_pairs(0, n)
+        for n in range(len(units)):
+            round_pairs(1, n)
+            turn_back(n)
+        woven_chunks = PAIRED // CHUNK
+        last = len(units) - 1
+        for n in range(last):
+            place(n, 0, units[n][1])
+        for b in range(2):
+            place(last, b, b + 1)
         weave("vector", 0)
-        for k in range(T // CHUNK):
-            if k + 2 < first_turned:
-                weave("vector", k + 1)
-            quantize_y(k)
+        for k in range(T // CHUNK - 1):
+            if k < woven_chunks:
+                weave("vector", k + 1, 0, min(CHUNK, PAIRED - (k + 1) * CHUNK))
+            quantize_y(k * CHUNK, (k + 1) * CHUNK)
+        for c0 in (T - 2 * P, T - P):
+            quantize_y(c0, c0 + P)
 
         out_scales = out_2.bitcast(I32).rearrange("g (q b) (a c) -> (g q) a b c", b=4, a=4)
         for q in range(P // 32):

@@ -25,6 +25,7 @@ RUN = 4
 HALF = N // 2
 CHUNK = 256
 PAIRED = 1152
+SCALAR_WEAVE = 64
 STORES = (768, 1536, 2048)
 
 DY_SCALAR = 256
@@ -262,6 +263,7 @@ def tile_attend_gfilm_c_pl_kernel(tc, dy, x, wg, wb, offs, out_0, out_1, out_2):
             round_pairs(1, n)
             turn_back(n)
         woven_chunks = PAIRED // CHUNK
+        weave("scalar", woven_chunks, PAIRED % CHUNK - SCALAR_WEAVE, PAIRED % CHUNK)
         last = len(units) - 1
         for n in range(last):
             place(n, 0, units[n][1])
@@ -270,7 +272,7 @@ def tile_attend_gfilm_c_pl_kernel(tc, dy, x, wg, wb, offs, out_0, out_1, out_2):
         weave("vector", 0)
         for k in range(T // CHUNK - 1):
             if k < woven_chunks:
-                weave("vector", k + 1, 0, min(CHUNK, PAIRED - (k + 1) * CHUNK))
+                weave("vector", k + 1, 0, min(CHUNK, PAIRED - SCALAR_WEAVE - (k + 1) * CHUNK))
             quantize_y(k * CHUNK, (k + 1) * CHUNK)
         for c0 in (T - 2 * P, T - P):
             quantize_y(c0, c0 + P)

@@ -25,7 +25,6 @@ RUN = 4
 HALF = N // 2
 CHUNK = 256
 PAIRED = 1152
-SCALAR_WEAVE = 64
 STORES = (768, 1536, 2048)
 
 DY_SCALAR = 256
@@ -174,7 +173,8 @@ def tile_attend_gfilm_c_pl_kernel(tc, dy, x, wg, wb, offs, out_0, out_1, out_2):
         scatter_half("scalar", 0, 1, sums0b[:])
         store(0)
         sums3 = sb.tile([P, N], F32, name="sums3")
-        nc.vector.tensor_copy(out=sums3[:], in_=banks[5][:])
+        nc.vector.tensor_copy(out=sums3[:, second], in_=banks[5][:, second])
+        nc.scalar.copy(out=sums3[:, first], in_=banks[5][:, first])
         scatter_half("vector", 1, 1, sums1b[:])
         store(1)
         nc.vector.tensor_copy(out=windows[3][:].indirect(offsets[:]), in_=sums3[:])
@@ -263,7 +263,6 @@ def tile_attend_gfilm_c_pl_kernel(tc, dy, x, wg, wb, offs, out_0, out_1, out_2):
             round_pairs(1, n)
             turn_back(n)
         woven_chunks = PAIRED // CHUNK
-        weave("scalar", woven_chunks, PAIRED % CHUNK - SCALAR_WEAVE, PAIRED % CHUNK)
         last = len(units) - 1
         for n in range(last):
             place(n, 0, units[n][1])
@@ -272,7 +271,7 @@ def tile_attend_gfilm_c_pl_kernel(tc, dy, x, wg, wb, offs, out_0, out_1, out_2):
         weave("vector", 0)
         for k in range(T // CHUNK - 1):
             if k < woven_chunks:
-                weave("vector", k + 1, 0, min(CHUNK, PAIRED - SCALAR_WEAVE - (k + 1) * CHUNK))
+                weave("vector", k + 1, 0, min(CHUNK, PAIRED - (k + 1) * CHUNK))
             quantize_y(k * CHUNK, (k + 1) * CHUNK)
         for c0 in (T - 2 * P, T - P):
             quantize_y(c0, c0 + P)

@@ -56,12 +56,14 @@ def tile_attend_gfilm_c_pl_kernel(tc, dy, x, wg, wb, offs, out_0, out_1, out_2):
         identity = sb.tile([P, P], F32, name="identity")
         make_identity(nc, identity[:])
 
-        windows = []
-        for n in range(3):
-            window = sb.tile([P, T], F32, name="window%d" % n)
-            clear = nc.gpsimd if n == 2 else nc.vector
-            clear.memset(window[:].bitcast(I32), 0)
-            windows.append(window)
+        windows = {}
+        for n in range(LANES):
+            windows[n] = sb.tile([P, T], F32, name="window%d" % n)
+            if n < 2:
+                for cols in (slice(0, T // 2 - 1), slice(T // 2 - 1, T)):
+                    nc.vector.memset(windows[n][:, cols].bitcast(I32), 0)
+            else:
+                nc.gpsimd.memset(windows[n][:].bitcast(I32), 0)
 
         def runs(rows):
             return rows.rearrange("p j (c i) -> p c j i", i=RUN)
@@ -159,8 +161,6 @@ def tile_attend_gfilm_c_pl_kernel(tc, dy, x, wg, wb, offs, out_0, out_1, out_2):
         sums1a = sb.tile([P, HALF], F32, name="x_second", align_bytes=64)
         nc.vector.tensor_copy(out=sums1a[:], in_=banks[2][:, first])
         quantize_dg(1, second)
-        windows.append(sb.tile([P, T], F32, name="dg_bf1", align_bytes=64))
-        nc.gpsimd.memset(windows[3][:].bitcast(I32), 0)
         scatter_half("vector", 1, 0, sums1a[:])
         for t in range(2):
             product(banks[2 * t + 1][:, first], t, 1, second)
@@ -213,7 +213,7 @@ def tile_attend_gfilm_c_pl_kernel(tc, dy, x, wg, wb, offs, out_0, out_1, out_2):
 
         units = ((PAIRED, 1), (1280, 2), (1536, 2), (1792, 2))
         first_banks = ("bank4", "bank6", "bank7", "bank2")
-        later_banks = ("bank1", "bank4", "bank6", "bank7")
+        later_banks = ("bank1", "bank3", "bank5", "bank0")
         across, staged, back = {}, {}, {}
 
         def turn_lane(t, n):
@@ -229,11 +229,11 @@ def tile_attend_gfilm_c_pl_kernel(tc, dy, x, wg, wb, offs, out_0, out_1, out_2):
             nc.scalar.copy(out=staged[u, n][:].rearrange("c b (p e) -> c b p e", e=2),
                            in_=across[u, n][:].rearrange("c b e p -> c b p e"))
 
-        def turn_back(n):
-            back[n] = psum.tile([P, units[n][1], 2, P], F32, name=later_banks[n])
-            for u in range(2):
-                for b in range(units[n][1]):
-                    nc.tensor.transpose(back[n][:, b, u, :], staged[u, n][:, b, :].bitcast(F32), identity[:])
+        def turn_back(u, n):
+            if n not in back:
+                back[n] = psum.tile([P, units[n][1], 2, P], F32, name=first_banks[n])
+            for b in range(units[n][1]):
+                nc.tensor.transpose(back[n][:, b, u, :], staged[u, n][:, b, :].bitcast(F32), identity[:])
 
         def place(n, b0, b1):
             c0 = units[n][0]
@@ -254,14 +254,16 @@ def tile_attend_gfilm_c_pl_kernel(tc, dy, x, wg, wb, offs, out_0, out_1, out_2):
         pair("vector", 3, 0, PAIRED)
         pair("vector", 2, 0, PAIRED // 2)
         pair("vector", 2, PAIRED // 2, PAIRED)
+        for t in (3, 2):
+            for n in range(len(units)):
+                turn_lane(t, n)
         for n in range(len(units)):
-            turn_lane(3, n)
-            turn_lane(2, n)
             if n:
                 round_pairs(0, n)
+            turn_back(0, n)
         for n in range(len(units)):
             round_pairs(1, n)
-            turn_back(n)
+            turn_back(1, n)
         woven_chunks = PAIRED // CHUNK
         last = len(units) - 1
         for n in range(last):

from contextlib import ExitStack

import concourse.mybir as mybir
from concourse.masks import make_identity

F = 512
D = 512
N = 512
T = 2048

FLOPS = 2 * 2 * F * D * N

F32 = mybir.dt.float32
BF16 = mybir.dt.bfloat16
I32 = mybir.dt.int32
U32 = mybir.dt.uint32
U16 = mybir.dt.uint16
U8 = mybir.dt.uint8
E4M3 = mybir.dt.float8_e4m3fn_x4
E5M2 = mybir.dt.float8_e5m2_x4

P = 128
LANES = 4
RUN = 4
HALF = N // 2
CHUNK = 256
PAIRED = 1152
STORES = (768, 1536, 2048)

DY_SCALAR = 256
WB_VECTOR = 56
WG_EARLY_VECTOR = 80
WG_LATE_VECTOR = 32


def tile_attend_gfilm_c_pl_kernel(tc, dy, x, wg, wb, offs, out_0, out_1, out_2):
    nc = tc.nc
    copy = {"vector": nc.vector.tensor_copy, "scalar": nc.scalar.copy}
    with ExitStack() as ctx:
        sb = ctx.enter_context(tc.tile_pool(name="sb", bufs=1))
        psum = ctx.enter_context(tc.psum_pool(name="psum", bufs=1))

        def load(src, name, c0, c1, queue=nc.sync):
            raw = sb.tile([P, LANES, c1 - c0], F32, name=name, align_bytes=64)
            queue.dma_start(out=raw[:], in_=src.rearrange("(p j) c -> p j c", j=LANES)[:, :, c0:c1])
            return raw

        dy_raw = load(dy, "dy_raw", 0, N)
        x_first = load(x, "x_first", 0, HALF, nc.scalar)
        wb_raw = load(wb, "wb_raw", 0, D)
        wg_raw = load(wg, "wg_raw", 0, D)
        x_second = load(x, "x_second", HALF, N)
        offsets = sb.tile([P, N // 16], U16, name="offsets")
        nc.sync.dma_start(offsets[:], offs)

        identity = sb.tile([P, P], F32, name="identity")
        make_identity(nc, identity[:])

        windows = {}
        for n in range(LANES):
            windows[n] = sb.tile([P, T], F32, name="window%d" % n)
            if n < 2:
                for cols in (slice(0, T // 2 - 1), slice(T // 2 - 1, T)):
                    nc.vector.memset(windows[n][:, cols].bitcast(I32), 0)
            else:
                nc.gpsimd.memset(windows[n][:].bitcast(I32), 0)

        def runs(rows):
            return rows.rearrange("p j (c i) -> p c j i", i=RUN)

        def woven(values):
            return values.rearrange("p (c i j) -> p c j i", i=RUN, j=LANES)

        def mx_tiles(words, name):
            codes = sb.tile([P, words], U32, name=name + "_codes", align_bytes=64)
            scales = sb.tile([P, words], U8, name=name + "_scales", align_bytes=64)
            return codes, scales

        def quantize(mx, values, fmt, c0, c1):
            nc.vector.quantize_mx(out=mx[0][:, c0:c1].bitcast(fmt), scales=mx[1][:, c0:c1],
                                  in_=values[:, LANES * c0:LANES * c1])

        dy_bf = sb.tile([P, N * LANES], BF16, name="dy_bf", align_bytes=64)
        dg_bf = [sb.tile([P, HALF * LANES], BF16, name="dg_bf%d" % h, align_bytes=64) for h in range(2)]
        dy_mx = mx_tiles(N, "dy")
        dg_mx = mx_tiles(N, "dg")
        first, second, whole = slice(0, HALF), slice(HALF, N), slice(0, N)
        nc.scalar.copy(out=woven(dy_bf[:, :LANES * DY_SCALAR]), in_=runs(dy_raw[:, :, :DY_SCALAR]))
        nc.vector.tensor_copy(out=woven(dy_bf[:, LANES * DY_SCALAR:]), in_=runs(dy_raw[:, :, DY_SCALAR:]))

        def multiply(h, x_raw, samples):
            nc.vector.tensor_tensor(out=woven(dg_bf[h][:]), in0=runs(dy_raw[:, :, samples]), in1=runs(x_raw[:]),
                                    op=mybir.AluOpType.mult)

        def quantize_dg(h, samples):
            nc.vector.quantize_mx(out=dg_mx[0][:, samples].bitcast(E5M2), scales=dg_mx[1][:, samples], in_=dg_bf[h][:])

        multiply(0, x_first, first)
        quantize(dy_mx, dy_bf, E5M2, 0, N)
        quantize_dg(0, first)

        w_bf = [sb.tile([P, D * LANES], BF16, name="w_bf%d" % u, align_bytes=64) for u in range(2)]
        w_mx = [mx_tiles(D, "w%d" % u) for u in range(2)]

        def deal(engine, raw, s, t0, t1, m0, m1):
            u = t0 // 2
            dealt = w_bf[u][:].rearrange("p (s e m j) -> p s m j e", s=2, e=2, j=LANES)
            src = raw[:].rearrange("p j (m t) -> p m j t", t=LANES)
            copy[engine](out=dealt[:, s, m0:m1, :, t0 - 2 * u:t1 - 2 * u], in_=src[:, m0:m1, :, t0:t1])

        for t0 in (0, 2):
            deal("vector", wb_raw, 0, t0, t0 + 2, 0, WB_VECTOR)
            deal("scalar", wb_raw, 0, t0, t0 + 2, WB_VECTOR, P)
        for u in range(2):
            quantize(w_mx[u], w_bf[u], E4M3, 0, 2 * P)
        for t0, m in ((0, WG_EARLY_VECTOR), (2, WG_LATE_VECTOR)):
            deal("vector", wg_raw, 1, t0, t0 + 2, 0, m)
            deal("scalar", wg_raw, 1, t0, t0 + 2, m, P)
            if t0 == 0:
                quantize(w_mx[0], w_bf[0], E4M3, 2 * P, 3 * P)
                quantize(w_mx[0], w_bf[0], E4M3, 3 * P, 4 * P)
        quantize(w_mx[1], w_bf[1], E4M3, 2 * P, 4 * P)

        def product(out, t, s, samples, closes=True):
            codes, scales = w_mx[t // 2]
            moving = (dy_mx, dg_mx)[s]
            cols = slice((2 * s + t % 2) * P, (2 * s + t % 2 + 1) * P)
            nc.tensor.matmul_mx(out=out, lhsT=codes[:, cols].bitcast(E4M3), lhsT_scale=scales[:, cols],
                                rhs=moving[0][:, samples].bitcast(E5M2), rhs_scale=moving[1][:, samples],
                                start=(s == 0), stop=(s == 1 and closes))

        banks = {b: psum.tile([P, N], F32, name="bank%d" % b) for b in (0, 1, 2, 3, 5)}
        for t in range(2):
            product(banks[2 * t][:, first], t, 0, first)
        for t in range(2):
            product(banks[2 * t + 1][:, first], t, 0, second)
        product(banks[5][:], 3, 0, whole)
        for t in range(2):
            product(banks[2 * t][:, first], t, 1, first)
        product(banks[5][:, first], 3, 1, first, closes=False)

        out_rows = out_0.rearrange("(p t) c -> p t c", t=LANES)

        def scatter_half(engine, t, h, src):
            window = windows[t][:].indirect(offsets[:, 16 * h:16 * (h + 1)])
            if engine == "scalar":
                nc.scalar.activation(out=window, in_=src, func=mybir.ActivationFunctionType.Copy)
            else:
                nc.vector.tensor_copy(out=window, in_=src)

        def store(t):
            nc.sync.dma_start(out=out_rows[:, t, :], in_=windows[t][:])

        sums0a = sb.tile([P, HALF], F32, name="sums0a")
        nc.scalar.copy(out=sums0a[:], in_=banks[0][:, first])
        banks[4] = psum.tile([P, N], F32, name="bank0")
        product(banks[4][:], 2, 0, whole)
        product(banks[4][:, first], 2, 1, first, closes=False)
        scatter_half("scalar", 0, 0, sums0a[:])
        multiply(1, x_second, second)
        sums1a = sb.tile([P, HALF], F32, name="x_second", align_bytes=64)
        nc.vector.tensor_copy(out=sums1a[:], in_=banks[2][:, first])
        quantize_dg(1, second)
        scatter_half("vector", 1, 0, sums1a[:])
        for t in range(2):
            product(banks[2 * t + 1][:, first], t, 1, second)
        for t in (3, 2):
            product(banks[2 + t][:, second], t, 1, second)
        sums0b = sb.tile([P, HALF], F32, name="sums0b")
        nc.scalar.copy(out=sums0b[:], in_=banks[1][:, first])
        sums1b = sb.tile([P, HALF], F32, name="sums1b")
        nc.scalar.copy(out=sums1b[:], in_=banks[3][:, first])
        scatter_half("scalar", 0, 1, sums0b[:])
        store(0)
        sums3 = sb.tile([P, N], F32, name="sums3")
        nc.vector.tensor_copy(out=sums3[:, second], in_=banks[5][:, second])
        nc.scalar.copy(out=sums3[:, first], in_=banks[5][:, first])
        scatter_half("vector", 1, 1, sums1b[:])
        store(1)
        nc.vector.tensor_copy(out=windows[3][:].indirect(offsets[:]), in_=sums3[:])
        store(3)
        sums2a = sb.tile([P, HALF], F32, name="sums2a", align_bytes=64)
        nc.scalar.copy(out=sums2a[:], in_=banks[4][:, first])
        sums2b = sb.tile([P, HALF], F32, name="sums2b")
        nc.scalar.copy(out=sums2b[:], in_=banks[4][:, second])
        scatter_half("scalar", 2, 0, sums2a[:])

        y_codes = sb.tile([P, T], U32, name="y_codes", align_bytes=64)
        y_scales = sb.tile([P, T // 4], U8, name="y_scales", align_bytes=64)
        y_bf = [sb.tile([P, CHUNK * LANES], BF16, name="y_bf%d" % k, align_bytes=64) for k in range(T // CHUNK)]
        copy["gpsimd"] = nc.gpsimd.tensor_copy
        out_words = out_1.rearrange("a p c l -> p (a c l)").bitcast(I32)

        def quantize_y(c0, c1):
            a, s0 = divmod(c0, T // 4)
            k, first_col = divmod(c0, CHUNK)
            nc.vector.quantize_mx(out=y_codes[:, c0:c1].bitcast(E4M3), scales=y_scales[4 * a:, s0:s0 + c1 - c0],
                                  in_=y_bf[k][:, LANES * first_col:LANES * (first_col + c1 - c0)])
            if c1 in STORES:
                start = ((0,) + STORES)[STORES.index(c1)]
                nc.sync.dma_start(out=out_words[:, start:c1], in_=y_codes[:, start:c1].bitcast(I32))

        pairs = sb.tile([P, LANES * PAIRED], BF16, name="pairs", align_bytes=64)

        def pair(engine, t, c0, c1):
            dst = pairs[:].rearrange("p (u c e) -> p u e c", u=2, e=2)[:, t // 2, t % 2, c0:c1]
            copy[engine](out=dst, in_=windows[t][:, c0:c1])

        def weave(engine, k, c0=0, c1=CHUNK):
            word = I32 if engine == "vector" else U32
            src = pairs[:].bitcast(word).rearrange("p (u c) -> p c u", u=2)[:, k * CHUNK + c0:k * CHUNK + c1]
            copy[engine](out=y_bf[k][:].bitcast(word).rearrange("p (c u) -> p c u", u=2)[:, c0:c1], in_=src)

        units = ((PAIRED, 1), (1280, 2), (1536, 2), (1792, 2))
        first_banks = ("bank4", "bank6", "bank7", "bank2")
        later_banks = ("bank1", "bank3", "bank5", "bank0")
        across, staged, back = {}, {}, {}

        def turn_lane(t, n):
            c0, blocks = units[n]
            if (t // 2, n) not in across:
                across[t // 2, n] = psum.tile([P, blocks, 2, P], F32, name=(first_banks, later_banks)[t // 2][n])
            for b in range(blocks):
                nc.tensor.transpose(across[t // 2, n][:, b, t % 2, :], windows[t][:, c0 + b * P:c0 + (b + 1) * P],
                                    identity[:])

        def round_pairs(u, n):
            staged[u, n] = sb.tile([P, units[n][1], 2 * P], BF16, name="staged%d_%d" % (u, n), align_bytes=64)
            nc.scalar.copy(out=staged[u, n][:].rearrange("c b (p e) -> c b p e", e=2),
                           in_=across[u, n][:].rearrange("c b e p -> c b p e"))

        def turn_back(u, n):
            if n not in back:
                back[n] = psum.tile([P, units[n][1], 2, P], F32, name=first_banks[n])
            for b in range(units[n][1]):
                nc.tensor.transpose(back[n][:, b, u, :], staged[u, n][:, b, :].bitcast(F32), identity[:])

        def place(n, b0, b1):
            c0 = units[n][0]
            values = y_bf[c0 // CHUNK][:, LANES * (c0 % CHUNK):]
            nc.scalar.copy(out=values.bitcast(F32).rearrange("p (b c u) -> p b c u", c=P, u=2)[:, b0:b1],
                           in_=back[n][:].rearrange("p b u c -> p b c u")[:, b0:b1])

        for t in range(2):
            turn_lane(t, 0)
        round_pairs(0, 0)
        scatter_half("scalar", 2, 1, sums2b[:])
        store(2)
        for t in range(2):
            pair("gpsimd", t, 0, PAIRED)
        for t in range(2):
            for n in range(1, len(units)):
                turn_lane(t, n)
        pair("vector", 3, 0, PAIRED)
        pair("vector", 2, 0, PAIRED // 2)
        pair("vector", 2, PAIRED // 2, PAIRED)
        for t in (3, 2):
            for n in range(len(units)):
                turn_lane(t, n)
        for n in range(len(units)):
            if n:
                round_pairs(0, n)
            turn_back(0, n)
        for n in range(len(units)):
            round_pairs(1, n)
            turn_back(1, n)
        woven_chunks = PAIRED // CHUNK
        last = len(units) - 1
        for n in range(last):
            place(n, 0, units[n][1])
        for b in range(2):
            place(last, b, b + 1)
        weave("vector", 0)
        for k in range(T // CHUNK - 1):
            if k < woven_chunks:
                weave("vector", k + 1, 0, min(CHUNK, PAIRED - (k + 1) * CHUNK))
            quantize_y(k * CHUNK, (k + 1) * CHUNK)
        for c0 in (T - 2 * P, T - P):
            quantize_y(c0, c0 + P)

        out_scales = out_2.bitcast(I32).rearrange("g (q b) (a c) -> (g q) a b c", b=4, a=4)
        for q in range(P // 32):
            queue = nc.scalar if q % 2 == 0 else nc.sync
            queue.dma_start(out=out_scales[q], in_=y_scales[32 * q:32 * q + 16, :].bitcast(I32))
